import numpy as np
import ml_dtypes


def mxq(x, axis, fmt="e4m3"):
    dtype, down = {"e4m3": (ml_dtypes.float8_e4m3fn, 7), "e5m2": (ml_dtypes.float8_e5m2, 14)}[fmt]
    v = np.moveaxis(np.asarray(x, np.float32).astype(ml_dtypes.bfloat16).astype(np.float64), axis, -1)
    blocks = v.reshape(v.shape[:-1] + (-1, 32))
    amax = np.abs(blocks).max(-1, keepdims=True)
    byte = np.maximum(np.where(amax > 0, np.frexp(amax)[1] - 1 + 127, 0) - down, 1)
    scale = np.exp2(byte - 127.0)
    codes = (blocks / scale).astype(np.float32).astype(dtype).astype(np.float64)
    return np.moveaxis((codes * scale).reshape(v.shape), -1, axis)


WIDE = False


def mx_kscale(k):
    if not WIDE:
        return np.ones(k)
    levels = np.array([10, -10, 5, -5, 0])
    if k % 512:
        return np.exp2(np.random.permutation(np.resize(levels, k // 32))).repeat(32)
    a = np.empty((k // 512, 16))
    for p in range(k // 512):
        a[p, :8] = np.random.permutation(np.resize(levels, 8))
        for g in range(8):
            far = levels[np.abs(levels - a[p, g]) >= 10]
            a[p, g + 8] = far[np.random.randint(len(far))]
    return np.exp2(a.ravel()).repeat(32)


BF16 = ml_dtypes.bfloat16


def bf(x):
    return np.asarray(x, np.float32).astype(BF16)


def f64(x):
    return np.asarray(x).astype(np.float64)


E2M1 = np.array([0.0, 0.5, 1.0, 1.5, 2.0, 3.0, 4.0, 6.0, -0.0, -0.5, -1.0, -1.5, -2.0, -3.0, -4.0, -6.0])


def pack_weight(w, fmt):
    k, n = w.shape
    w = f64(bf(w)).reshape(k // 32, 32, n)
    amax = np.abs(w).max(1)
    if fmt == "e4m3":
        byte = np.frexp(amax)[1] - 1 + 127 - 7
    else:
        mant, ex = np.frexp(amax / 6.0)
        byte = np.where(mant > 0.5, ex, ex - 1) + 127
    byte = np.clip(np.where(amax > 0, byte, 1), 1, 254)
    scaled = (w * np.exp2(127.0 - byte)[:, None, :]).reshape(k, n).astype(np.float32)
    by_word = np.ascontiguousarray(scaled.reshape(k // 512, 128, 4, n).transpose(0, 1, 3, 2))
    if fmt == "e4m3":
        words = by_word.astype(ml_dtypes.float8_e4m3fn).view(np.uint8)
    else:
        c = by_word.astype(ml_dtypes.float4_e2m1fn).view(np.uint8) & 0xF
        words = c[..., 0::2] | (c[..., 1::2] << 4)
    return np.ascontiguousarray(words), np.ascontiguousarray(byte.astype(np.uint8).reshape(k // 512, 16, n))


def unpack_weight(words, scales, fmt):
    g, p, n, _ = words.shape
    if fmt == "e4m3":
        vals = np.ascontiguousarray(words).view(ml_dtypes.float8_e4m3fn).astype(np.float64)
    else:
        nib = np.empty((g, p, n, 4), np.uint8)
        nib[..., 0::2] = words & 0xF
        nib[..., 1::2] = words >> 4
        vals = E2M1[nib]
    vals = vals * np.repeat(np.exp2(scales.astype(np.float64) - 127.0), 8, axis=1)[..., None]
    return vals.transpose(0, 1, 3, 2).reshape(g * 512, n)
def pack4(w):
    words, scales = pack_weight(w, "e2m1")
    return words.reshape(words.shape[0], 128, -1), scales


def unpack4(words, scales):
    return unpack_weight(words.reshape(words.shape[0], 128, -1, 2), scales, "e2m1")


T, J, P, R, Q = 256, 4, 512, 512, 1024


def draw0():
    g, u = mx_kscale(P), mx_kscale(R)
    x = bf(np.random.standard_normal((T, J, P)) * g)
    a = bf(np.random.standard_normal((J, J)) / np.sqrt(J))
    b = bf(np.random.standard_normal((P, R)) / np.sqrt(P) / g[:, None] * u[None, :])
    e = bf(1.0 + 0.1 * np.random.standard_normal(R))
    c_words, c_scales = pack4(np.random.standard_normal((R, Q)) / np.sqrt(R) / u[:, None])
    s = bf(1.0 + 0.1 * np.random.standard_normal(Q))
    return {"x": x,
            "a": a,
            "b": b,
            "e": e,
            "c_words": c_words,
            "c_scales": c_scales,
            "s": s}


def mix_blocks(a, z):
    m = a[:, 0][None, :, None] * z[:, 0, :][:, None, :]
    for j in range(1, a.shape[1]):
        m = m + a[:, j][None, :, None] * z[:, j, :][:, None, :]
    return m


def core(x, a, b, e, c_words, c_scales, s):
    x, a, b, e, s = f64(x), f64(a), f64(b), f64(e), f64(s)
    c = unpack4(c_words, c_scales)
    t, j, p = x.shape
    q = c.shape[1]
    be = b * e[None, :]
    w2 = mxq(be, 1, "e4m3") @ c
    z = (mxq(x.reshape(t * j, p), 1, "e4m3") @ mxq(w2, 0, "e4m3")).reshape(t, j, q)
    m = mix_blocks(a, z)
    return m * s[None, None, :]


def e4m3fn_bytes(y):
    return np.clip(np.asarray(y, np.float64), -448.0, 448.0).astype(np.float32).astype(ml_dtypes.float8_e4m3fn).view(np.uint8)


def e4m3fn_values(b):
    return np.asarray(b, np.uint8).view(ml_dtypes.float8_e4m3fn).astype(np.float64)


def setup_inputs():
    d = draw0()
    x0 = np.asarray(d['x']).astype(np.float64)
    s = (np.max(np.abs(x0), axis=(0, 1), keepdims=True) / 448.0).astype(np.float32)
    out = {}
    for k, v in d.items():
        if k == 'x':
            out['x_bytes'] = e4m3fn_bytes(x0 / s.astype(np.float64))
            out['x_scale'] = s
        else:
            out[k] = v
    return out


def reference(x_bytes, x_scale, a, b, e, c_words, c_scales, s):
    return core(e4m3fn_values(x_bytes) * x_scale.astype(np.float64), a, b, e, c_words, c_scales, s)

@@ -1,0 +1,509 @@
+from contextlib import ExitStack
+
+import concourse.mybir as mybir
+from concourse.masks import make_identity
+
+T, J, KP, R, Q = 256, 4, 512, 512, 1024
+FLOPS = 2 * KP * R * Q + 2 * T * J * KP * Q + 2 * T * J * J * Q
+
+F32 = mybir.dt.float32
+BF16 = mybir.dt.bfloat16
+I32 = mybir.dt.int32
+U32 = mybir.dt.uint32
+U8 = mybir.dt.uint8
+FP8 = mybir.dt.float8_e4m3fn
+FP8X4 = mybir.dt.float8_e4m3fn_x4
+FP4X4 = mybir.dt.float4_e2m1fn_x4
+MULT = mybir.AluOpType.mult
+ADD = mybir.AluOpType.add
+COPY = mybir.ActivationFunctionType.Copy
+AXIS_X = mybir.AxisListType.X
+ENGINE = mybir.EngineType
+
+P = 128
+HALF = 512
+BANKS = 8
+
+
+def tile_lokrrankgatedkroneckerdelta_w4_kernel(
+    tc, x_bytes, x_scale, a, b, e, c_words, c_scales, s, out
+):
+    nc = tc.nc
+    with ExitStack() as ctx:
+        sb = ctx.enter_context(tc.tile_pool(name="sb", bufs=1))
+        ps = ctx.enter_context(tc.psum_pool(name="ps", bufs=1))
+
+        def new(name, shape, dtype):
+            return sb.tile(shape, dtype, name=name, align_bytes=64)
+
+        free_banks = list(range(BANKS))
+
+        def take_bank():
+            k = free_banks[0]
+            free_banks.remove(k)
+            return k, ps.tile([P, HALF], F32, name="bank%d" % k, tag="bank%d" % k)
+
+        def give_bank(k):
+            free_banks.append(k)
+
+        ident = new("ident", [P, P], F32)
+        same_token = new("same_token", [P, 32], F32)
+        mixer = new("mixer", [P, P], F32)
+        pick = new("pick", [P, J], F32)
+        a_bf = new("a_bf", [P, J * J], BF16)
+        a_all = new("a_all", [P, J * J], F32)
+        a_picked = new("a_picked", [P, J, J], F32)
+        a_col = new("a_col", [P, J], F32)
+        e_col = new("e_col", [P, 2, 2], BF16)
+        xs_col = new("xs_col", [P, 4], F32)
+        xs_all = new("xs_all", [P, KP], F32)
+        s_all = new("s_all", [P, Q], BF16)
+        b_rows = [new("b_rows%d" % h, [P, 2, R], BF16) for h in range(2)]
+        cw = new("cw", [P, 2 * Q], U8)
+        csc = new("csc", [P, Q], U8)
+        xm_bytes = new("xm_bytes", [P, 4, KP], U8)
+        xe_bytes = new("xe_bytes", [P, 4, KP], U8)
+        be = [new("be%d" % t, [P, R], BF16) for t in range(4)]
+        be_t = [new("be_t%d" % t, [P, R], BF16) for t in range(4)]
+        be_codes = new("be_codes", [P, KP], U32)
+        be_scales = new("be_scales", [P, KP], U8)
+        xb = [new("xb%d" % r, [P, KP], BF16) for r in range(8)]
+        x_t = [new("x_t%d" % g, [P, 2 * KP], BF16) for g in range(2)]
+        xm_t = new("xm_t", [P, 4 * KP], BF16)
+        dup_codes = new("dup_codes", [P, HALF], U32)
+        dup_scales = new("dup_scales", [P, HALF], U8)
+        x_codes = new("x_codes", [P, T * J], U32)
+        x_scales = new("x_scales", [P, T * J], U8)
+        w2b = [new("w2b%d" % g, [P, 1024], BF16) for g in range(2)]
+        w2b_late = new("w2b_late", [P, 2048], BF16)
+        w2_codes = new("w2_codes", [P, Q], U32)
+        w2_scales = new("w2_scales", [P, Q], U8)
+        z_sb = [new("z_sb%d" % n, [P, HALF], F32) for n in range(10)]
+        out_m = [new("out_m%d" % n, [P, HALF], F32) for n in range(10)]
+        out_e = [new("out_e%d" % n, [P, 2, HALF], F32) for n in range(4)]
+
+        make_identity(nc, ident[:])
+
+        ordered = set([ENGINE.PE, ENGINE.Activation, ENGINE.DVE, ENGINE.Pool])
+        ctx.enter_context(tc.manual_schedule(engines=ordered))
+        nc.vector.memset(csc[:].bitcast(I32), 0)
+        nc.sync.dma_start(out=e_col[:], in_=e.rearrange("(w p k) -> p w k", p=P, k=2))
+        nc.scalar.dma_start(out=xs_col[:], in_=x_scale.rearrange("o u (p m) -> p (o u m)", m=4))
+        nc.scalar.dma_start(out=a_bf[:], in_=a.rearrange("i j -> (i j)").partition_broadcast(P))
+        b_view = b.rearrange("(m t) r -> m t r", t=4)
+        for h in range(2):
+            nc.sync.dma_start(out=b_rows[h][:], in_=b_view[:, 2 * h : 2 * h + 2, :])
+        nc.sync.dma_start(out=xm_bytes[:], in_=x_bytes[0 : P])
+        nc.sync.dma_start(out=cw[:].bitcast(I32), in_=c_words[0].bitcast(I32))
+        for quad in range(4):
+            nc.sync.dma_start(
+                out=csc[32 * quad : 32 * quad + 4, :].bitcast(I32),
+                in_=c_scales[0, 4 * quad : 4 * quad + 4, :].bitcast(I32),
+            )
+        nc.sync.dma_start(out=xe_bytes[:], in_=x_bytes[P : 2 * P])
+        nc.sync.dma_start(out=s_all[:], in_=s.partition_broadcast(P))
+
+        nc.vector.tensor_reduce(
+            out=pick[:], in_=ident[:].rearrange("p (j t) -> p j t", j=J), axis=AXIS_X, op=ADD
+        )
+        nc.vector.tensor_reduce(
+            out=same_token[:], in_=ident[:].rearrange("p (j t) -> p t j", j=J), axis=AXIS_X, op=ADD
+        )
+        nc.scalar.activation(out=a_all[:], in_=a_bf[:], func=COPY)
+
+        e_bank_n, e_bank = take_bank()
+        e_words = e_col[:].rearrange("p w k -> p (w k)").bitcast(F32)
+        for w in range(2):
+            nc.tensor.transpose(
+                e_bank[:, w * P : (w + 1) * P], e_words[:, w : w + 1].to_broadcast([P, P]), ident[:]
+            )
+        xs_bank_n, xs_bank = take_bank()
+        for m in range(4):
+            nc.tensor.transpose(
+                xs_bank[:, m * P : (m + 1) * P], xs_col[:, m : m + 1].to_broadcast([P, P]), ident[:]
+            )
+        nc.scalar.copy(
+            out=xs_all[:].rearrange("p (n m) -> p n m", m=4),
+            in_=xs_bank[:].rearrange("p (m n) -> p n m", m=4),
+        )
+        give_bank(xs_bank_n)
+
+        def pick_a():
+            nc.vector.tensor_tensor(
+                out=a_picked[:],
+                in0=a_bf[:].rearrange("p (i j) -> p i j", j=J),
+                in1=pick[:].unsqueeze(1).to_broadcast([P, J, J]),
+                op=MULT,
+            )
+
+        def sum_a():
+            nc.vector.tensor_reduce(out=a_col[:], in_=a_picked[:], axis=AXIS_X, op=ADD)
+
+        def build_mixer():
+            nc.vector.tensor_tensor(
+                out=mixer[:].rearrange("p (t i) -> p t i", i=J),
+                in0=same_token[:].unsqueeze(2).to_broadcast([P, P // J, J]),
+                in1=a_col[:].unsqueeze(1).to_broadcast([P, P // J, J]),
+                op=MULT,
+            )
+
+        def turn(rows, bank, slot):
+            words = rows[:].bitcast(F32)
+            for u in range(2):
+                c0 = (2 * slot + u) * P
+                nc.tensor.transpose(bank[:, c0 : c0 + P], words[:, u : 2 * P : 2], ident[:])
+
+        def gate_b(t):
+            nc.vector.tensor_tensor(
+                out=be[t][:], in0=b_rows[t // 2][:, t % 2, :], in1=e_bank[:, 0 : 2 * P].bitcast(BF16), op=MULT
+            )
+
+        def turn_be(t):
+            k, bank = take_bank()
+            turn(be[t], bank, 0)
+            nc.scalar.copy(
+                out=be_t[t][:].bitcast(F32).rearrange("p (r u) -> p r u", u=2),
+                in_=bank[:, 0 : 2 * P].rearrange("p (u r) -> p r u", u=2),
+            )
+            give_bank(k)
+
+        def quantize(src, codes, scales, c0, n):
+            nc.vector.quantize_mx(
+                out=codes[:, c0 : c0 + n].bitcast(FP8X4), scales=scales[:, c0 : c0 + n], in_=src
+            )
+
+        def quantize_be(t):
+            quantize(be_t[t][:], be_codes, be_scales, t * P, P)
+
+        def scale_x(r):
+            src = xm_bytes if r < 4 else xe_bytes
+            nc.vector.tensor_tensor(out=xb[r][:], in0=src[:, r % 4, :].bitcast(FP8), in1=xs_all[:], op=MULT)
+
+        turned = {}
+
+        def turn_x(g):
+            k, bank = take_bank()
+            for slot in range(2):
+                turn(xb[2 * g + slot], bank, slot)
+            turned.setdefault(g, (k, bank))
+
+        def copy_x(g, on_vector=False):
+            k, bank = turned[g]
+            move = nc.vector.tensor_copy if on_vector else nc.scalar.copy
+            if g < 2:
+                move(
+                    out=xm_t[:].bitcast(F32).rearrange("p (r j t u) -> p j r t u", r=4, j=J, u=2)[:, 2 * g : 2 * g + 2],
+                    in_=bank[:].rearrange("p (a u r t) -> p a r t u", a=2, u=2, r=4),
+                )
+            else:
+                move(
+                    out=x_t[g - 2][:].bitcast(F32).rearrange("p (a r u) -> p a r u", a=2, u=2),
+                    in_=bank[:].rearrange("p (a u r) -> p a r u", a=2, u=2),
+                )
+            give_bank(k)
+
+        def quantize_x(g):
+            src = xm_t[:, 2 * g * KP : 2 * (g + 1) * KP] if g < 2 else x_t[g - 2][:]
+            quantize(src, x_codes, x_scales, 2 * g * P, 2 * P)
+
+        def regroup_codes():
+            nc.vector.tensor_copy(
+                out=dup_codes[:].rearrange("p (r j t) -> p r j t", r=4, j=J),
+                in_=x_codes[:, HALF:].rearrange("p (j r t) -> p r j t", r=4, j=J),
+            )
+            nc.vector.tensor_copy(
+                out=dup_scales[:].bitcast(U32).rearrange("p (r j t) -> p r j t", r=4, j=J),
+                in_=x_scales[:, HALF:].bitcast(U32).rearrange("p (j r t) -> p r j t", r=4, j=J),
+            )
+
+        w2_banks = {}
+
+        def make_w2(c):
+            k, bank = take_bank()
+            for t in range(4):
+                nc.tensor.matmul_mx(
+                    out=bank[:, t * P : (t + 1) * P],
+                    lhsT=be_codes[:, t * P : (t + 1) * P].bitcast(FP8X4),
+                    lhsT_scale=be_scales[:, t * P : (t + 1) * P],
+                    rhs=cw[:, 2 * c * P : 2 * (c + 1) * P].bitcast(FP4X4),
+                    rhs_scale=csc[:, c * P : (c + 1) * P],
+                    start=True,
+                    stop=True,
+                )
+            w2_banks.setdefault(c, (k, bank))
+
+        def copy_w2(c, on_vector=False):
+            k, bank = w2_banks[c]
+            move = nc.vector.tensor_copy if on_vector else nc.scalar.copy
+            if c < 4:
+                dst = w2b[c // 2][:, (c % 2) * HALF : (c % 2 + 1) * HALF]
+            else:
+                dst = w2b_late[:, (c - 4) * HALF : (c - 3) * HALF]
+            move(
+                out=dst.rearrange("p (n t) -> p n t", t=4),
+                in_=bank[:].rearrange("p (t n) -> p n t", t=4),
+            )
+            give_bank(k)
+
+        def quantize_w2(g):
+            quantize(w2b[g][:], w2_codes, w2_scales, 2 * g * P, 2 * P)
+
+        def quantize_w2_late():
+            quantize(w2b_late[:], w2_codes, w2_scales, HALF, HALF)
+
+        def product(r, h):
+            k, bank = take_bank()
+            cols = slice(r * P, (r + 1) * P)
+            q_cols = slice(h * HALF, (h + 1) * HALF)
+            nc.tensor.matmul_mx(
+                out=bank[:],
+                lhsT=x_codes[:, cols].bitcast(FP8X4),
+                lhsT_scale=x_scales[:, cols],
+                rhs=w2_codes[:, q_cols].bitcast(FP8X4),
+                rhs_scale=w2_scales[:, q_cols],
+                start=True,
+                stop=True,
+            )
+            return k, bank
+
+        out_rows = out.rearrange("t i q -> (t i) q")
+        raw = {}
+        mixed = {}
+
+        extra = {8: (Q - P, P), 9: (Q - P - 64, 64)}
+
+        def s_of(n):
+            if n in extra:
+                q0, w = extra[n]
+                return s_all[:, q0 : q0 + w].unsqueeze(1).to_broadcast([P, 4, w])
+            return s_all[:, (n // 4) * HALF : (n // 4 + 1) * HALF]
+
+        def used(n, ap):
+            return ap[:, 0 : 4 * extra[n][1]] if n in extra else ap[:]
+
+        def shaped(n, ap):
+            return used(n, ap).rearrange("p (r q) -> p r q", r=4) if n in extra else ap[:]
+
+        def m_product(n):
+            if n < 8:
+                raw.setdefault(n, product(n % 4, n // 4))
+                return
+            k, bank = take_bank()
+            q1 = extra[n][0] + extra[n][1]
+            for r in range(4):
+                cols = slice(r * P, (r + 1) * P)
+                nc.tensor.matmul_mx(
+                    out=bank[:, cols],
+                    lhsT=dup_codes[:, cols].bitcast(FP8X4),
+                    lhsT_scale=dup_scales[:, cols],
+                    rhs=w2_codes[:, q1 - P : q1].bitcast(FP8X4),
+                    rhs_scale=w2_scales[:, q1 - P : q1],
+                    start=True,
+                    stop=True,
+                )
+            raw.setdefault(n, (k, bank))
+
+        def m_copy(n):
+            k, bank = raw[n]
+            src = bank[:]
+            if n in extra:
+                src = src.rearrange("p (r q) -> p r q", r=4)[:, :, P - extra[n][1] :]
+            nc.scalar.copy(out=shaped(n, z_sb[n]), in_=src)
+            give_bank(k)
+
+        def m_scale(n):
+            nc.gpsimd.tensor_tensor(out=shaped(n, z_sb[n]), in0=shaped(n, z_sb[n]), in1=s_of(n), op=MULT)
+
+        def m_mix(n):
+            k, bank = take_bank()
+            nc.tensor.matmul(used(n, bank), lhsT=mixer[:], rhs=used(n, z_sb[n]), start=True, stop=True)
+            mixed.setdefault(n, (k, bank))
+
+        def m_out(n, on_vector=False, late=False):
+            h, r = divmod(n, 4)
+            k, bank = mixed[n]
+            if on_vector:
+                nc.vector.tensor_tensor(out=shaped(n, out_m[n]), in0=shaped(n, bank), in1=s_of(n), op=MULT)
+            else:
+                nc.scalar.copy(out=used(n, out_m[n]), in_=used(n, bank))
+            give_bank(k)
+            if late:
+                nc.gpsimd.tensor_tensor(out=shaped(n, out_m[n]), in0=shaped(n, out_m[n]), in1=s_of(n), op=MULT)
+            if n in extra:
+                q0, w = extra[n]
+                dst = out_rows[4 * P :, q0 : q0 + w].rearrange("(r p) q -> p r q", p=P)
+            else:
+                dst = out_rows[r * P : (r + 1) * P, h * HALF : (h + 1) * HALF]
+            nc.sync.dma_start(out=dst, in_=shaped(n, out_m[n]))
+
+        e_banks = {}
+        widths = [HALF, HALF - P - 64]
+
+        def e_product(h, j):
+            e_banks.setdefault((h, j), product(4 + j, h))
+
+        def acc(h, i):
+            return out_e[2 * h + i // 2][:, i % 2, 0 : widths[h]]
+
+        def e_first(h, i):
+            k, bank = e_banks[(h, 0)]
+            nc.scalar.activation(
+                out=acc(h, i), in_=bank[:, 0 : widths[h]], func=COPY, scale=a_all[:, J * i : J * i + 1]
+            )
+
+        def e_add(h, i, j):
+            k, bank = e_banks[(h, j)]
+            nc.vector.scalar_tensor_tensor(
+                out=acc(h, i), in0=bank[:, 0 : widths[h]], scalar=a_all[:, J * i + j : J * i + j + 1],
+                in1=acc(h, i), op0=MULT, op1=ADD,
+            )
+
+        def e_pair(h, pair, js=(1, 2, 3)):
+            for j in js:
+                for i in range(2 * pair, 2 * pair + 2):
+                    e_add(h, i, j)
+
+        def e_done(h, j):
+            give_bank(e_banks[(h, j)][0])
+
+        def e_last(h, pair, engine):
+            sums = out_e[2 * h + pair][:, :, 0 : widths[h]]
+            s_cols = s_all[:, h * HALF : h * HALF + widths[h]]
+            engine.tensor_tensor(
+                out=sums, in0=sums, in1=s_cols.unsqueeze(1).to_broadcast([P, 2, widths[h]]), op=MULT
+            )
+            nc.sync.dma_start(
+                out=out[P : 2 * P, 2 * pair : 2 * pair + 2, h * HALF : h * HALF + widths[h]], in_=sums
+            )
+
+        def e_one(h, i, engine):
+            s_cols = s_all[:, h * HALF : h * HALF + widths[h]]
+            engine.tensor_tensor(out=acc(h, i), in0=acc(h, i), in1=s_cols, op=MULT)
+            nc.sync.dma_start(out=out[P : 2 * P, i, h * HALF : h * HALF + widths[h]], in_=acc(h, i))
+
+        pick_a()
+        sum_a()
+        build_mixer()
+        for t in range(4):
+            gate_b(t)
+            turn_be(t)
+        give_bank(e_bank_n)
+        quantize_be(0)
+        scale_x(0)
+        quantize_be(1)
+        quantize_be(2)
+        quantize_be(3)
+        scale_x(1)
+        make_w2(0)
+        make_w2(1)
+        turn_x(0)
+        make_w2(2)
+        make_w2(3)
+        scale_x(2)
+        scale_x(3)
+        copy_w2(0)
+        copy_w2(1)
+        turn_x(1)
+        scale_x(4)
+        copy_x(0)
+        quantize_w2(0)
+        scale_x(5)
+        copy_w2(2)
+        copy_w2(3)
+        turn_x(2)
+        make_w2(4)
+        make_w2(5)
+        scale_x(6)
+        copy_x(1)
+        quantize_w2(1)
+        scale_x(7)
+        copy_x(2)
+        make_w2(6)
+        make_w2(7)
+        quantize_x(0)
+        turn_x(3)
+        quantize_x(2)
+        copy_w2(4)
+        copy_w2(6, True)
+        m_product(0)
+        e_product(0, 0)
+        quantize_x(1)
+        copy_x(3)
+        copy_w2(5)
+        copy_w2(7, True)
+        m_product(1)
+        e_product(0, 1)
+        quantize_x(3)
+        m_copy(0)
+        m_mix(0)
+        quantize_w2_late()
+        regroup_codes()
+        e_first(0, 0)
+        e_first(0, 1)
+        e_product(0, 2)
+        e_product(0, 3)
+        m_copy(1)
+        m_product(2)
+        m_mix(1)
+        m_out(0, False, True)
+        m_copy(2)
+        m_product(3)
+        m_mix(2)
+        e_pair(0, 0)
+        e_last(0, 0, nc.gpsimd)
+        e_first(0, 2)
+        m_copy(3)
+        e_first(0, 3)
+        e_done(0, 0)
+        m_product(4)
+        m_out(1, False, True)
+        m_mix(3)
+        e_pair(0, 1, (1,))
+        e_done(0, 1)
+        m_out(2, True)
+        m_copy(4)
+        m_product(5)
+        e_product(1, 0)
+        m_mix(4)
+        m_out(3, False, True)
+        e_pair(0, 1, (2,))
+        e_done(0, 2)
+        e_first(1, 0)
+        e_first(1, 1)
+        m_copy(5)
+        e_product(1, 1)
+        e_product(1, 2)
+        m_product(6)
+        e_pair(0, 1, (3,))
+        e_done(0, 3)
+        e_last(0, 1, nc.gpsimd)
+        m_mix(5)
+        m_out(4, True)
+        e_first(1, 2)
+        e_first(1, 3)
+        e_done(1, 0)
+        m_copy(6)
+        e_product(1, 3)
+        m_product(7)
+        m_mix(6)
+        e_pair(1, 0, (1, 2))
+        m_out(5, True)
+        e_pair(1, 0, (3,))
+        e_last(1, 0, nc.gpsimd)
+        m_copy(7)
+        m_product(8)
+        m_mix(7)
+        m_out(6, False, True)
+        m_copy(8)
+        m_product(9)
+        m_mix(8)
+        m_copy(9)
+        e_pair(1, 1, (1, 2))
+        e_done(1, 1)
+        m_mix(9)
+        m_out(7, True)
+        e_pair(1, 1, (3,))
+        m_out(8, True)
+        e_one(1, 2, nc.vector)
+        e_one(1, 3, nc.vector)
+        m_out(9, True)

@@ -21,8 +21,15 @@ AXIS_X = mybir.AxisListType.X
 ENGINE = mybir.EngineType
 
 P = 128
-HALF = 512
+PACK = 4
+BANK = 512
 BANKS = 8
+GROUP = P // J
+GROUPS = P // GROUP
+
+LATE_UNITS = ((Q - P, P), (Q - P - 64, 64))
+CHAIN_RANGES = ((0, BANK), (BANK, LATE_UNITS[1][0] - BANK))
+UNITS_ON_GPSIMD = 3
 
 
 def tile_lokrrankgatedkroneckerdelta_w4_kernel(
@@ -30,369 +37,320 @@ def tile_lokrrankgatedkroneckerdelta_w4_kernel(
 ):
     nc = tc.nc
     with ExitStack() as ctx:
-        sb = ctx.enter_context(tc.tile_pool(name="sb", bufs=1))
-        ps = ctx.enter_context(tc.psum_pool(name="ps", bufs=1))
+        sbuf = ctx.enter_context(tc.tile_pool(name="sbuf", bufs=1))
+        psum = ctx.enter_context(tc.psum_pool(name="psum", bufs=1))
 
         def new(name, shape, dtype):
-            return sb.tile(shape, dtype, name=name, align_bytes=64)
+            return sbuf.tile(shape, dtype, name=name, align_bytes=64)
 
         free_banks = list(range(BANKS))
+        held = {}
 
-        def take_bank():
-            k = free_banks[0]
-            free_banks.remove(k)
-            return k, ps.tile([P, HALF], F32, name="bank%d" % k, tag="bank%d" % k)
+        def take_bank(use):
+            number = free_banks[0]
+            free_banks.remove(number)
+            bank = psum.tile([P, BANK], F32, name="bank%d" % number, tag="bank%d" % number)
+            held.setdefault(use, (number, bank))
+            return bank
 
-        def give_bank(k):
-            free_banks.append(k)
+        def bank_of(use):
+            return held[use][1]
+
+        def give_bank(use):
+            free_banks.append(held[use][0])
 
         ident = new("ident", [P, P], F32)
-        same_token = new("same_token", [P, 32], F32)
-        mixer = new("mixer", [P, P], F32)
-        pick = new("pick", [P, J], F32)
+        same_token = new("same_token", [P, GROUP], F32)
+        same_block = new("same_block", [P, J], F32)
         a_bf = new("a_bf", [P, J * J], BF16)
         a_all = new("a_all", [P, J * J], F32)
-        a_picked = new("a_picked", [P, J, J], F32)
+        a_masked = new("a_masked", [P, J, J], F32)
         a_col = new("a_col", [P, J], F32)
-        e_col = new("e_col", [P, 2, 2], BF16)
-        xs_col = new("xs_col", [P, 4], F32)
+        mixer = new("mixer", [P, P], F32)
+        e_pairs = new("e_pairs", [P, 2, 2], BF16)
+        xs_col = new("xs_col", [P, PACK], F32)
         xs_all = new("xs_all", [P, KP], F32)
         s_all = new("s_all", [P, Q], BF16)
-        b_rows = [new("b_rows%d" % h, [P, 2, R], BF16) for h in range(2)]
-        cw = new("cw", [P, 2 * Q], U8)
-        csc = new("csc", [P, Q], U8)
-        xm_bytes = new("xm_bytes", [P, 4, KP], U8)
-        xe_bytes = new("xe_bytes", [P, 4, KP], U8)
-        be = [new("be%d" % t, [P, R], BF16) for t in range(4)]
-        be_t = [new("be_t%d" % t, [P, R], BF16) for t in range(4)]
+        b_rows = [new("b_rows%d" % t, [P, R], BF16) for t in range(PACK)]
+        be_rows = [new("be_rows%d" % t, [P, R], BF16) for t in range(PACK)]
+        be_turned = [new("be_turned%d" % t, [P, R], BF16) for t in range(PACK)]
         be_codes = new("be_codes", [P, KP], U32)
         be_scales = new("be_scales", [P, KP], U8)
-        xb = [new("xb%d" % r, [P, KP], BF16) for r in range(8)]
-        x_t = [new("x_t%d" % g, [P, 2 * KP], BF16) for g in range(2)]
-        xm_t = new("xm_t", [P, 4 * KP], BF16)
-        dup_codes = new("dup_codes", [P, HALF], U32)
-        dup_scales = new("dup_scales", [P, HALF], U8)
+        c_codes = new("c_codes", [P, 2 * Q], U8)
+        c_plane = new("c_plane", [P, Q], U8)
+        x_raw = [new("x_raw%d" % half, [P, J, KP], U8) for half in range(2)]
+        x_rows = [new("x_rows%d" % n, [P, KP], BF16) for n in range(2 * J)]
+        x_turned_matrix = new("x_turned_matrix", [P, J * KP], BF16)
+        x_turned_chain = [new("x_turned_chain%d" % n, [P, 2 * KP], BF16) for n in range(2)]
         x_codes = new("x_codes", [P, T * J], U32)
         x_scales = new("x_scales", [P, T * J], U8)
-        w2b = [new("w2b%d" % g, [P, 1024], BF16) for g in range(2)]
-        w2b_late = new("w2b_late", [P, 2048], BF16)
+        late_codes = new("late_codes", [P, P * J], U32)
+        late_scales = new("late_scales", [P, P * J], U8)
+        w2_early = [new("w2_early%d" % n, [P, 2 * BANK], BF16) for n in range(2)]
+        w2_late = new("w2_late", [P, 4 * BANK], BF16)
         w2_codes = new("w2_codes", [P, Q], U32)
         w2_scales = new("w2_scales", [P, Q], U8)
-        z_sb = [new("z_sb%d" % n, [P, HALF], F32) for n in range(10)]
-        out_m = [new("out_m%d" % n, [P, HALF], F32) for n in range(10)]
-        out_e = [new("out_e%d" % n, [P, 2, HALF], F32) for n in range(4)]
+        units = 2 * GROUPS + len(LATE_UNITS)
+        unit_z = [new("unit_z%d" % n, [P, BANK], F32) for n in range(units)]
+        unit_out = [new("unit_out%d" % n, [P, BANK], F32) for n in range(units)]
+        chains = [(half, i) for half in range(2) for i in range(J)]
+        chain_sum = [new("chain_sum%d" % n, [P, CHAIN_RANGES[n // J][1]], F32) for n in range(len(chains))]
 
         make_identity(nc, ident[:])
+        ctx.enter_context(tc.manual_schedule(engines=set([ENGINE.PE, ENGINE.Activation, ENGINE.DVE, ENGINE.Pool])))
 
-        ordered = set([ENGINE.PE, ENGINE.Activation, ENGINE.DVE, ENGINE.Pool])
-        ctx.enter_context(tc.manual_schedule(engines=ordered))
-        nc.vector.memset(csc[:].bitcast(I32), 0)
-        nc.sync.dma_start(out=e_col[:], in_=e.rearrange("(w p k) -> p w k", p=P, k=2))
-        nc.scalar.dma_start(out=xs_col[:], in_=x_scale.rearrange("o u (p m) -> p (o u m)", m=4))
+        nc.vector.memset(c_plane[:].bitcast(I32), 0)
+        nc.sync.dma_start(out=e_pairs[:], in_=e.rearrange("(w n k) -> n w k", n=P, k=2))
+        nc.scalar.dma_start(out=xs_col[:], in_=x_scale.rearrange("o u (n m) -> n (o u m)", m=PACK))
         nc.scalar.dma_start(out=a_bf[:], in_=a.rearrange("i j -> (i j)").partition_broadcast(P))
-        b_view = b.rearrange("(m t) r -> m t r", t=4)
-        for h in range(2):
-            nc.sync.dma_start(out=b_rows[h][:], in_=b_view[:, 2 * h : 2 * h + 2, :])
-        nc.sync.dma_start(out=xm_bytes[:], in_=x_bytes[0 : P])
-        nc.sync.dma_start(out=cw[:].bitcast(I32), in_=c_words[0].bitcast(I32))
-        for quad in range(4):
+        for t in range(PACK):
+            nc.sync.dma_start(out=b_rows[t][:], in_=b.rearrange("(m t) r -> m t r", t=PACK)[:, t, :])
+        nc.sync.dma_start(out=x_raw[0][:], in_=x_bytes[0:P])
+        nc.sync.dma_start(out=c_codes[:].bitcast(I32), in_=c_words[0].bitcast(I32))
+        for g in range(4):
             nc.sync.dma_start(
-                out=csc[32 * quad : 32 * quad + 4, :].bitcast(I32),
-                in_=c_scales[0, 4 * quad : 4 * quad + 4, :].bitcast(I32),
+                out=c_plane[32 * g : 32 * g + 4, :].bitcast(I32),
+                in_=c_scales[0, 4 * g : 4 * g + 4, :].bitcast(I32),
             )
-        nc.sync.dma_start(out=xe_bytes[:], in_=x_bytes[P : 2 * P])
-        nc.sync.dma_start(out=s_all[:], in_=s.partition_broadcast(P))
+        nc.sync.dma_start(out=x_raw[1][:], in_=x_bytes[P : 2 * P])
 
         nc.vector.tensor_reduce(
-            out=pick[:], in_=ident[:].rearrange("p (j t) -> p j t", j=J), axis=AXIS_X, op=ADD
+            out=same_block[:], in_=ident[:].rearrange("n (j t) -> n j t", j=J), axis=AXIS_X, op=ADD
         )
         nc.vector.tensor_reduce(
-            out=same_token[:], in_=ident[:].rearrange("p (j t) -> p t j", j=J), axis=AXIS_X, op=ADD
+            out=same_token[:], in_=ident[:].rearrange("n (j t) -> n t j", j=J), axis=AXIS_X, op=ADD
         )
-        nc.scalar.activation(out=a_all[:], in_=a_bf[:], func=COPY)
 
-        e_bank_n, e_bank = take_bank()
-        e_words = e_col[:].rearrange("p w k -> p (w k)").bitcast(F32)
-        for w in range(2):
-            nc.tensor.transpose(
-                e_bank[:, w * P : (w + 1) * P], e_words[:, w : w + 1].to_broadcast([P, P]), ident[:]
-            )
-        xs_bank_n, xs_bank = take_bank()
-        for m in range(4):
-            nc.tensor.transpose(
-                xs_bank[:, m * P : (m + 1) * P], xs_col[:, m : m + 1].to_broadcast([P, P]), ident[:]
-            )
-        nc.scalar.copy(
-            out=xs_all[:].rearrange("p (n m) -> p n m", m=4),
-            in_=xs_bank[:].rearrange("p (m n) -> p n m", m=4),
+        def spread(bank, columns, count):
+            for m in range(count):
+                nc.tensor.transpose(
+                    bank[:, m * P : (m + 1) * P], columns[:, m : m + 1].to_broadcast([P, P]), ident[:]
+                )
+
+        spread(take_bank("e"), e_pairs[:].rearrange("n w k -> n (w k)").bitcast(F32), 2)
+        spread(take_bank("xs"), xs_col[:], PACK)
+        nc.scalar.activation(
+            out=xs_all[:].rearrange("n (k m) -> n k m", m=PACK),
+            in_=bank_of("xs")[:].rearrange("n (m k) -> n k m", m=PACK),
+            func=COPY,
         )
-        give_bank(xs_bank_n)
+        give_bank("xs")
 
-        def pick_a():
+        def mask_a():
             nc.vector.tensor_tensor(
-                out=a_picked[:],
-                in0=a_bf[:].rearrange("p (i j) -> p i j", j=J),
-                in1=pick[:].unsqueeze(1).to_broadcast([P, J, J]),
+                out=a_masked[:],
+                in0=a_bf[:].rearrange("n (i j) -> n i j", j=J),
+                in1=same_block[:].unsqueeze(1).to_broadcast([P, J, J]),
                 op=MULT,
             )
 
-        def sum_a():
-            nc.vector.tensor_reduce(out=a_col[:], in_=a_picked[:], axis=AXIS_X, op=ADD)
+        def pick_a():
+            nc.vector.tensor_reduce(out=a_col[:], in_=a_masked[:], axis=AXIS_X, op=ADD)
 
         def build_mixer():
             nc.vector.tensor_tensor(
-                out=mixer[:].rearrange("p (t i) -> p t i", i=J),
-                in0=same_token[:].unsqueeze(2).to_broadcast([P, P // J, J]),
-                in1=a_col[:].unsqueeze(1).to_broadcast([P, P // J, J]),
+                out=mixer[:].rearrange("n (t i) -> n t i", i=J),
+                in0=same_token[:].unsqueeze(2).to_broadcast([P, GROUP, J]),
+                in1=a_col[:].unsqueeze(1).to_broadcast([P, GROUP, J]),
                 op=MULT,
             )
 
         def turn(rows, bank, slot):
             words = rows[:].bitcast(F32)
             for u in range(2):
-                c0 = (2 * slot + u) * P
-                nc.tensor.transpose(bank[:, c0 : c0 + P], words[:, u : 2 * P : 2], ident[:])
+                first = (2 * slot + u) * P
+                nc.tensor.transpose(bank[:, first : first + P], words[:, u : 2 * P : 2], ident[:])
 
-        def gate_b(t):
-            nc.vector.tensor_tensor(
-                out=be[t][:], in0=b_rows[t // 2][:, t % 2, :], in1=e_bank[:, 0 : 2 * P].bitcast(BF16), op=MULT
-            )
-
-        def turn_be(t):
-            k, bank = take_bank()
-            turn(be[t], bank, 0)
-            nc.scalar.copy(
-                out=be_t[t][:].bitcast(F32).rearrange("p (r u) -> p r u", u=2),
-                in_=bank[:, 0 : 2 * P].rearrange("p (u r) -> p r u", u=2),
-            )
-            give_bank(k)
-
-        def quantize(src, codes, scales, c0, n):
+        def quantize(src, codes, scales, first, count):
             nc.vector.quantize_mx(
-                out=codes[:, c0 : c0 + n].bitcast(FP8X4), scales=scales[:, c0 : c0 + n], in_=src
+                out=codes[:, first : first + count].bitcast(FP8X4), scales=scales[:, first : first + count], in_=src
             )
+
+        def gate_and_turn_b(t):
+            nc.vector.tensor_tensor(
+                out=be_rows[t][:], in0=b_rows[t][:], in1=bank_of("e")[:, 0 : R // 2].bitcast(BF16), op=MULT
+            )
+            bank = take_bank(("be", t))
+            turn(be_rows[t], bank, 0)
+            nc.scalar.copy(
+                out=be_turned[t][:].bitcast(F32).rearrange("n (m u) -> n m u", u=2),
+                in_=bank[:, 0 : 2 * P].rearrange("n (u m) -> n m u", u=2),
+            )
+            give_bank(("be", t))
 
         def quantize_be(t):
-            quantize(be_t[t][:], be_codes, be_scales, t * P, P)
-
-        def scale_x(r):
-            src = xm_bytes if r < 4 else xe_bytes
-            nc.vector.tensor_tensor(out=xb[r][:], in0=src[:, r % 4, :].bitcast(FP8), in1=xs_all[:], op=MULT)
-
-        turned = {}
-
-        def turn_x(g):
-            k, bank = take_bank()
-            for slot in range(2):
-                turn(xb[2 * g + slot], bank, slot)
-            turned.setdefault(g, (k, bank))
-
-        def copy_x(g, on_vector=False):
-            k, bank = turned[g]
-            move = nc.vector.tensor_copy if on_vector else nc.scalar.copy
-            if g < 2:
-                move(
-                    out=xm_t[:].bitcast(F32).rearrange("p (r j t u) -> p j r t u", r=4, j=J, u=2)[:, 2 * g : 2 * g + 2],
-                    in_=bank[:].rearrange("p (a u r t) -> p a r t u", a=2, u=2, r=4),
-                )
-            else:
-                move(
-                    out=x_t[g - 2][:].bitcast(F32).rearrange("p (a r u) -> p a r u", a=2, u=2),
-                    in_=bank[:].rearrange("p (a u r) -> p a r u", a=2, u=2),
-                )
-            give_bank(k)
-
-        def quantize_x(g):
-            src = xm_t[:, 2 * g * KP : 2 * (g + 1) * KP] if g < 2 else x_t[g - 2][:]
-            quantize(src, x_codes, x_scales, 2 * g * P, 2 * P)
-
-        def regroup_codes():
-            nc.vector.tensor_copy(
-                out=dup_codes[:].rearrange("p (r j t) -> p r j t", r=4, j=J),
-                in_=x_codes[:, HALF:].rearrange("p (j r t) -> p r j t", r=4, j=J),
-            )
-            nc.vector.tensor_copy(
-                out=dup_scales[:].bitcast(U32).rearrange("p (r j t) -> p r j t", r=4, j=J),
-                in_=x_scales[:, HALF:].bitcast(U32).rearrange("p (j r t) -> p r j t", r=4, j=J),
-            )
-
-        w2_banks = {}
+            quantize(be_turned[t][:], be_codes, be_scales, t * P, P)
 
         def make_w2(c):
-            k, bank = take_bank()
-            for t in range(4):
+            bank = take_bank(("w2", c))
+            for t in range(PACK):
                 nc.tensor.matmul_mx(
                     out=bank[:, t * P : (t + 1) * P],
                     lhsT=be_codes[:, t * P : (t + 1) * P].bitcast(FP8X4),
                     lhsT_scale=be_scales[:, t * P : (t + 1) * P],
-                    rhs=cw[:, 2 * c * P : 2 * (c + 1) * P].bitcast(FP4X4),
-                    rhs_scale=csc[:, c * P : (c + 1) * P],
+                    rhs=c_codes[:, 2 * c * P : 2 * (c + 1) * P].bitcast(FP4X4),
+                    rhs_scale=c_plane[:, c * P : (c + 1) * P],
                     start=True,
                     stop=True,
                 )
-            w2_banks.setdefault(c, (k, bank))
 
-        def copy_w2(c, on_vector=False):
-            k, bank = w2_banks[c]
-            move = nc.vector.tensor_copy if on_vector else nc.scalar.copy
-            if c < 4:
-                dst = w2b[c // 2][:, (c % 2) * HALF : (c % 2 + 1) * HALF]
-            else:
-                dst = w2b_late[:, (c - 4) * HALF : (c - 3) * HALF]
-            move(
-                out=dst.rearrange("p (n t) -> p n t", t=4),
-                in_=bank[:].rearrange("p (t n) -> p n t", t=4),
+        def copy_w2(c, copy):
+            wide, slot = (w2_early[c // 2], c % 2) if c < 4 else (w2_late, c - 4)
+            copy(
+                out=wide[:, slot * BANK : (slot + 1) * BANK].rearrange("m (q t) -> m q t", t=PACK),
+                in_=bank_of(("w2", c))[:].rearrange("m (t q) -> m q t", t=PACK),
             )
-            give_bank(k)
+            give_bank(("w2", c))
 
-        def quantize_w2(g):
-            quantize(w2b[g][:], w2_codes, w2_scales, 2 * g * P, 2 * P)
+        def quantize_w2_early(n):
+            quantize(w2_early[n][:], w2_codes, w2_scales, 2 * n * P, 2 * P)
 
-        def quantize_w2_late():
-            quantize(w2b_late[:], w2_codes, w2_scales, HALF, HALF)
+        def scale_x(n):
+            nc.vector.tensor_tensor(
+                out=x_rows[n][:], in0=x_raw[n // J][:, n % J, :].bitcast(FP8), in1=xs_all[:], op=MULT
+            )
 
-        def product(r, h):
-            k, bank = take_bank()
-            cols = slice(r * P, (r + 1) * P)
-            q_cols = slice(h * HALF, (h + 1) * HALF)
+        def turn_x(pair):
+            bank = take_bank(("x", pair))
+            for slot in range(2):
+                turn(x_rows[2 * pair + slot], bank, slot)
+
+        def copy_x(pair, copy):
+            bank = bank_of(("x", pair))
+            if pair < 2:
+                wide = x_turned_matrix[:].bitcast(F32).rearrange("n (g j t u) -> n j g t u", g=GROUPS, j=J, u=2)
+                copy(
+                    out=wide[:, 2 * pair : 2 * pair + 2],
+                    in_=bank[:].rearrange("n (j u g t) -> n j g t u", j=2, u=2, g=GROUPS),
+                )
+            else:
+                copy(
+                    out=x_turned_chain[pair - 2][:].bitcast(F32).rearrange("n (j t u) -> n j t u", j=2, u=2),
+                    in_=bank[:].rearrange("n (j u t) -> n j t u", j=2, u=2),
+                )
+            give_bank(("x", pair))
+
+        def quantize_x(n):
+            src = x_turned_matrix[:, 2 * n * KP : 2 * (n + 1) * KP] if n < 2 else x_turned_chain[n - 2][:]
+            quantize(src, x_codes, x_scales, 2 * n * P, 2 * P)
+
+        def regroup_late_codes():
+            nc.vector.tensor_copy(
+                out=late_codes[:].rearrange("n (g j t) -> n g j t", g=GROUPS, j=J),
+                in_=x_codes[:, P * J :].rearrange("n (j g t) -> n g j t", g=GROUPS, j=J),
+            )
+            nc.vector.tensor_copy(
+                out=late_scales[:].bitcast(U32).rearrange("n (g j t) -> n g j t", g=GROUPS, j=J),
+                in_=x_scales[:, P * J :].bitcast(U32).rearrange("n (j g t) -> n g j t", g=GROUPS, j=J),
+            )
+
+        def second_product(dst, codes, scales, first, q_cols):
             nc.tensor.matmul_mx(
-                out=bank[:],
-                lhsT=x_codes[:, cols].bitcast(FP8X4),
-                lhsT_scale=x_scales[:, cols],
+                out=dst,
+                lhsT=codes[:, first : first + P].bitcast(FP8X4),
+                lhsT_scale=scales[:, first : first + P],
                 rhs=w2_codes[:, q_cols].bitcast(FP8X4),
                 rhs_scale=w2_scales[:, q_cols],
                 start=True,
                 stop=True,
             )
-            return k, bank
 
         out_rows = out.rearrange("t i q -> (t i) q")
-        raw = {}
-        mixed = {}
 
-        extra = {8: (Q - P, P), 9: (Q - P - 64, 64)}
+        def late(n):
+            return n >= 2 * GROUPS
 
-        def s_of(n):
-            if n in extra:
-                q0, w = extra[n]
-                return s_all[:, q0 : q0 + w].unsqueeze(1).to_broadcast([P, 4, w])
-            return s_all[:, (n // 4) * HALF : (n // 4 + 1) * HALF]
+        def q_range(n):
+            return LATE_UNITS[n - 2 * GROUPS] if late(n) else ((n // GROUPS) * BANK, BANK)
 
-        def used(n, ap):
-            return ap[:, 0 : 4 * extra[n][1]] if n in extra else ap[:]
+        def flat(n, buffer):
+            return buffer[:, 0 : GROUPS * q_range(n)[1]] if late(n) else buffer[:]
 
-        def shaped(n, ap):
-            return used(n, ap).rearrange("p (r q) -> p r q", r=4) if n in extra else ap[:]
+        def by_group(n, buffer):
+            return flat(n, buffer).rearrange("n (g q) -> n g q", g=GROUPS) if late(n) else buffer[:]
 
-        def m_product(n):
-            if n < 8:
-                raw.setdefault(n, product(n % 4, n // 4))
-                return
-            k, bank = take_bank()
-            q1 = extra[n][0] + extra[n][1]
-            for r in range(4):
-                cols = slice(r * P, (r + 1) * P)
-                nc.tensor.matmul_mx(
-                    out=bank[:, cols],
-                    lhsT=dup_codes[:, cols].bitcast(FP8X4),
-                    lhsT_scale=dup_scales[:, cols],
-                    rhs=w2_codes[:, q1 - P : q1].bitcast(FP8X4),
-                    rhs_scale=w2_scales[:, q1 - P : q1],
-                    start=True,
-                    stop=True,
+        def s_for_unit(n):
+            first, width = q_range(n)
+            s_cols = s_all[:, first : first + width]
+            return s_cols.unsqueeze(1).to_broadcast([P, GROUPS, width]) if late(n) else s_cols
+
+        def unit_product(n):
+            bank = take_bank(("z", n))
+            first, width = q_range(n)
+            if late(n):
+                for g in range(GROUPS):
+                    q_cols = slice(first + width - P, first + width)
+                    second_product(bank[:, g * P : (g + 1) * P], late_codes, late_scales, g * P, q_cols)
+            else:
+                second_product(bank[:], x_codes, x_scales, (n % GROUPS) * P, slice(first, first + width))
+
+        def unit_copy(n):
+            z = bank_of(("z", n))[:]
+            if late(n):
+                z = z.rearrange("n (g q) -> n g q", g=GROUPS)[:, :, P - q_range(n)[1] :]
+            nc.scalar.copy(out=by_group(n, unit_z[n]), in_=z)
+            give_bank(("z", n))
+
+        def unit_mix(n):
+            bank = take_bank(("mixed", n))
+            nc.tensor.matmul(flat(n, bank), lhsT=mixer[:], rhs=flat(n, unit_z[n]), start=True, stop=True)
+
+        def unit_finish(n):
+            bank = bank_of(("mixed", n))
+            result = by_group(n, unit_out[n])
+            if n < UNITS_ON_GPSIMD:
+                nc.scalar.copy(out=result, in_=by_group(n, bank))
+                nc.gpsimd.tensor_tensor(out=result, in0=result, in1=s_for_unit(n), op=MULT)
+            else:
+                nc.vector.tensor_tensor(out=result, in0=by_group(n, bank), in1=s_for_unit(n), op=MULT)
+            give_bank(("mixed", n))
+            first, width = q_range(n)
+            if late(n):
+                dst = out_rows[P * J :, first : first + width].rearrange("(g n) q -> n g q", n=P)
+            else:
+                dst = out_rows[(n % GROUPS) * P : (n % GROUPS + 1) * P, first : first + width]
+            nc.sync.dma_start(out=dst, in_=result)
+
+        def chain_product(half, j):
+            bank = take_bank(("zj", half, j))
+            second_product(bank[:], x_codes, x_scales, (J + j) * P, slice(half * BANK, (half + 1) * BANK))
+
+        def chain_term(n, j):
+            half, i = chains[n]
+            z = bank_of(("zj", half, j))[:, 0 : CHAIN_RANGES[half][1]]
+            weight = a_all[:, J * i + j : J * i + j + 1]
+            if j == 0:
+                nc.scalar.activation(out=chain_sum[n][:], in_=z, func=COPY, scale=weight)
+            else:
+                nc.vector.scalar_tensor_tensor(
+                    out=chain_sum[n][:], in0=z, scalar=weight, in1=chain_sum[n][:], op0=MULT, op1=ADD
                 )
-            raw.setdefault(n, (k, bank))
+            if i == J - 1:
+                give_bank(("zj", half, j))
 
-        def m_copy(n):
-            k, bank = raw[n]
-            src = bank[:]
-            if n in extra:
-                src = src.rearrange("p (r q) -> p r q", r=4)[:, :, P - extra[n][1] :]
-            nc.scalar.copy(out=shaped(n, z_sb[n]), in_=src)
-            give_bank(k)
-
-        def m_scale(n):
-            nc.gpsimd.tensor_tensor(out=shaped(n, z_sb[n]), in0=shaped(n, z_sb[n]), in1=s_of(n), op=MULT)
-
-        def m_mix(n):
-            k, bank = take_bank()
-            nc.tensor.matmul(used(n, bank), lhsT=mixer[:], rhs=used(n, z_sb[n]), start=True, stop=True)
-            mixed.setdefault(n, (k, bank))
-
-        def m_out(n, on_vector=False, late=False):
-            h, r = divmod(n, 4)
-            k, bank = mixed[n]
-            if on_vector:
-                nc.vector.tensor_tensor(out=shaped(n, out_m[n]), in0=shaped(n, bank), in1=s_of(n), op=MULT)
-            else:
-                nc.scalar.copy(out=used(n, out_m[n]), in_=used(n, bank))
-            give_bank(k)
-            if late:
-                nc.gpsimd.tensor_tensor(out=shaped(n, out_m[n]), in0=shaped(n, out_m[n]), in1=s_of(n), op=MULT)
-            if n in extra:
-                q0, w = extra[n]
-                dst = out_rows[4 * P :, q0 : q0 + w].rearrange("(r p) q -> p r q", p=P)
-            else:
-                dst = out_rows[r * P : (r + 1) * P, h * HALF : (h + 1) * HALF]
-            nc.sync.dma_start(out=dst, in_=shaped(n, out_m[n]))
-
-        e_banks = {}
-        widths = [HALF, HALF - P - 64]
-
-        def e_product(h, j):
-            e_banks.setdefault((h, j), product(4 + j, h))
-
-        def acc(h, i):
-            return out_e[2 * h + i // 2][:, i % 2, 0 : widths[h]]
-
-        def e_first(h, i):
-            k, bank = e_banks[(h, 0)]
-            nc.scalar.activation(
-                out=acc(h, i), in_=bank[:, 0 : widths[h]], func=COPY, scale=a_all[:, J * i : J * i + 1]
-            )
-
-        def e_add(h, i, j):
-            k, bank = e_banks[(h, j)]
-            nc.vector.scalar_tensor_tensor(
-                out=acc(h, i), in0=bank[:, 0 : widths[h]], scalar=a_all[:, J * i + j : J * i + j + 1],
-                in1=acc(h, i), op0=MULT, op1=ADD,
-            )
-
-        def e_pair(h, pair, js=(1, 2, 3)):
-            for j in js:
-                for i in range(2 * pair, 2 * pair + 2):
-                    e_add(h, i, j)
-
-        def e_done(h, j):
-            give_bank(e_banks[(h, j)][0])
-
-        def e_last(h, pair, engine):
-            sums = out_e[2 * h + pair][:, :, 0 : widths[h]]
-            s_cols = s_all[:, h * HALF : h * HALF + widths[h]]
+        def chain_finish(n):
+            half, i = chains[n]
+            first, width = CHAIN_RANGES[half]
+            engine = nc.vector if n == len(chains) - 1 else nc.gpsimd
             engine.tensor_tensor(
-                out=sums, in0=sums, in1=s_cols.unsqueeze(1).to_broadcast([P, 2, widths[h]]), op=MULT
+                out=chain_sum[n][:], in0=chain_sum[n][:], in1=s_all[:, first : first + width], op=MULT
             )
-            nc.sync.dma_start(
-                out=out[P : 2 * P, 2 * pair : 2 * pair + 2, h * HALF : h * HALF + widths[h]], in_=sums
-            )
+            nc.sync.dma_start(out=out[P : 2 * P, i, first : first + width], in_=chain_sum[n][:])
 
-        def e_one(h, i, engine):
-            s_cols = s_all[:, h * HALF : h * HALF + widths[h]]
-            engine.tensor_tensor(out=acc(h, i), in0=acc(h, i), in1=s_cols, op=MULT)
-            nc.sync.dma_start(out=out[P : 2 * P, i, h * HALF : h * HALF + widths[h]], in_=acc(h, i))
+        on_scalar = nc.scalar.copy
+        on_vector = nc.vector.tensor_copy
 
-        pick_a()
-        sum_a()
-        build_mixer()
-        for t in range(4):
-            gate_b(t)
-            turn_be(t)
-        give_bank(e_bank_n)
+        for t in range(PACK):
+            gate_and_turn_b(t)
+        give_bank("e")
+        mask_a()
         quantize_be(0)
+        pick_a()
         scale_x(0)
-        quantize_be(1)
-        quantize_be(2)
-        quantize_be(3)
+        for t in range(1, PACK):
+            quantize_be(t)
+        nc.scalar.activation(out=a_all[:], in_=a_bf[:], func=COPY)
+
         scale_x(1)
         make_w2(0)
         make_w2(1)
@@ -401,109 +359,66 @@ def tile_lokrrankgatedkroneckerdelta_w4_kernel(
         make_w2(3)
         scale_x(2)
         scale_x(3)
-        copy_w2(0)
-        copy_w2(1)
+        copy_w2(0, on_scalar)
+        copy_w2(1, on_scalar)
+        nc.scalar.dma_start(out=s_all[:], in_=s.partition_broadcast(P))
         turn_x(1)
         scale_x(4)
-        copy_x(0)
-        quantize_w2(0)
+        copy_x(0, on_scalar)
+        quantize_w2_early(0)
         scale_x(5)
-        copy_w2(2)
-        copy_w2(3)
+        copy_w2(2, on_scalar)
+        copy_w2(3, on_scalar)
         turn_x(2)
         make_w2(4)
         make_w2(5)
         scale_x(6)
-        copy_x(1)
-        quantize_w2(1)
+        build_mixer()
+        copy_x(1, on_scalar)
+        quantize_w2_early(1)
         scale_x(7)
-        copy_x(2)
+        copy_x(2, on_scalar)
+
         make_w2(6)
         make_w2(7)
         quantize_x(0)
         turn_x(3)
         quantize_x(2)
-        copy_w2(4)
-        copy_w2(6, True)
-        m_product(0)
-        e_product(0, 0)
+        copy_w2(4, on_scalar)
+        copy_w2(6, on_vector)
+        unit_product(0)
+        chain_product(0, 0)
+        copy_w2(7, on_vector)
+        copy_x(3, on_vector)
         quantize_x(1)
-        copy_x(3)
-        copy_w2(5)
-        copy_w2(7, True)
-        m_product(1)
-        e_product(0, 1)
+        copy_w2(5, on_scalar)
+        unit_product(1)
+        chain_product(0, 1)
         quantize_x(3)
-        m_copy(0)
-        m_mix(0)
-        quantize_w2_late()
-        regroup_codes()
-        e_first(0, 0)
-        e_first(0, 1)
-        e_product(0, 2)
-        e_product(0, 3)
-        m_copy(1)
-        m_product(2)
-        m_mix(1)
-        m_out(0, False, True)
-        m_copy(2)
-        m_product(3)
-        m_mix(2)
-        e_pair(0, 0)
-        e_last(0, 0, nc.gpsimd)
-        e_first(0, 2)
-        m_copy(3)
-        e_first(0, 3)
-        e_done(0, 0)
-        m_product(4)
-        m_out(1, False, True)
-        m_mix(3)
-        e_pair(0, 1, (1,))
-        e_done(0, 1)
-        m_out(2, True)
-        m_copy(4)
-        m_product(5)
-        e_product(1, 0)
-        m_mix(4)
-        m_out(3, False, True)
-        e_pair(0, 1, (2,))
-        e_done(0, 2)
-        e_first(1, 0)
-        e_first(1, 1)
-        m_copy(5)
-        e_product(1, 1)
-        e_product(1, 2)
-        m_product(6)
-        e_pair(0, 1, (3,))
-        e_done(0, 3)
-        e_last(0, 1, nc.gpsimd)
-        m_mix(5)
-        m_out(4, True)
-        e_first(1, 2)
-        e_first(1, 3)
-        e_done(1, 0)
-        m_copy(6)
-        e_product(1, 3)
-        m_product(7)
-        m_mix(6)
-        e_pair(1, 0, (1, 2))
-        m_out(5, True)
-        e_pair(1, 0, (3,))
-        e_last(1, 0, nc.gpsimd)
-        m_copy(7)
-        m_product(8)
-        m_mix(7)
-        m_out(6, False, True)
-        m_copy(8)
-        m_product(9)
-        m_mix(8)
-        m_copy(9)
-        e_pair(1, 1, (1, 2))
-        e_done(1, 1)
-        m_mix(9)
-        m_out(7, True)
-        e_pair(1, 1, (3,))
-        m_out(8, True)
-        e_one(1, 2, nc.vector)
-        e_one(1, 3, nc.vector)
-        m_out(9, True)
+        unit_copy(0)
+        unit_mix(0)
+        quantize(w2_late[:], w2_codes, w2_scales, BANK, BANK)
+        regroup_late_codes()
+        unit_copy(1)
+        chain_term(0, 0)
+        chain_term(1, 0)
+
+        for n in range(len(chains)):
+            if n + 2 < len(chains):
+                chain_product(*divmod(n + 2, J))
+            unit_product(n + 2)
+            unit_mix(n + 1)
+            unit_finish(n)
+            unit_copy(n + 2)
+            if n + 2 < len(chains):
+                chain_term(n + 2, 0)
+            chain_term(n, 1)
+            if n > 0:
+                chain_term(n - 1, 3)
+                chain_finish(n - 1)
+            chain_term(n, 2)
+        unit_mix(units - 1)
+        unit_finish(units - 2)
+        chain_term(len(chains) - 1, 3)
+        unit_finish(units - 1)
+        chain_finish(len(chains) - 1)

@@ -29,6 +29,7 @@ GROUPS = P // GROUP
 
 LATE_UNITS = ((Q - P, P), (Q - P - 64, 64))
 CHAIN_RANGES = ((0, BANK), (BANK, LATE_UNITS[1][0] - BANK))
+CHAIN_PASSES = (((0, BANK),), ((0, 2 * P), (2 * P, P)))
 UNITS_ON_GPSIMD = 3
 
 
@@ -84,8 +85,9 @@ def tile_lokrrankgatedkroneckerdelta_w4_kernel(
         x_turned_chain = [new("x_turned_chain%d" % n, [P, 2 * KP], BF16) for n in range(2)]
         x_codes = new("x_codes", [P, T * J], U32)
         x_scales = new("x_scales", [P, T * J], U8)
-        late_codes = new("late_codes", [P, P * J], U32)
-        late_scales = new("late_scales", [P, P * J], U8)
+        s_bf = new("s_bf", [P, len(LATE_UNITS), 2], BF16)
+        s_col = new("s_col", [P, len(LATE_UNITS)], F32)
+        late_zt = [new("late_zt%d" % n, [P, BANK], F32) for n in range(len(LATE_UNITS))]
         w2_early = [new("w2_early%d" % n, [P, 2 * BANK], BF16) for n in range(2)]
         w2_late = new("w2_late", [P, 4 * BANK], BF16)
         w2_codes = new("w2_codes", [P, Q], U32)
@@ -234,23 +236,16 @@ def tile_lokrrankgatedkroneckerdelta_w4_kernel(
             src = x_turned_matrix[:, 2 * n * KP : 2 * (n + 1) * KP] if n < 2 else x_turned_chain[n - 2][:]
             quantize(src, x_codes, x_scales, 2 * n * P, 2 * P)
 
-        def regroup_late_codes():
-            nc.vector.tensor_copy(
-                out=late_codes[:].rearrange("n (g j t) -> n g j t", g=GROUPS, j=J),
-                in_=x_codes[:, P * J :].rearrange("n (j g t) -> n g j t", g=GROUPS, j=J),
-            )
-            nc.vector.tensor_copy(
-                out=late_scales[:].bitcast(U32).rearrange("n (g j t) -> n g j t", g=GROUPS, j=J),
-                in_=x_scales[:, P * J :].bitcast(U32).rearrange("n (j g t) -> n g j t", g=GROUPS, j=J),
-            )
-
-        def second_product(dst, codes, scales, first, q_cols):
+        def second_product(dst, x_cols, q_cols, turned):
+            x_part = (x_codes[:, x_cols].bitcast(FP8X4), x_scales[:, x_cols])
+            w2_part = (w2_codes[:, q_cols].bitcast(FP8X4), w2_scales[:, q_cols])
+            stationary, moving = (w2_part, x_part) if turned else (x_part, w2_part)
             nc.tensor.matmul_mx(
                 out=dst,
-                lhsT=codes[:, first : first + P].bitcast(FP8X4),
-                lhsT_scale=scales[:, first : first + P],
-                rhs=w2_codes[:, q_cols].bitcast(FP8X4),
-                rhs_scale=w2_scales[:, q_cols],
+                lhsT=stationary[0],
+                lhsT_scale=stationary[1],
+                rhs=moving[0],
+                rhs_scale=moving[1],
                 start=True,
                 stop=True,
             )
@@ -269,20 +264,37 @@ def tile_lokrrankgatedkroneckerdelta_w4_kernel(
         def by_group(n, buffer):
             return flat(n, buffer).rearrange("n (g q) -> n g q", g=GROUPS) if late(n) else buffer[:]
 
-        def s_for_unit(n):
+        def late_chunk(n):
             first, width = q_range(n)
-            s_cols = s_all[:, first : first + width]
-            return s_cols.unsqueeze(1).to_broadcast([P, GROUPS, width]) if late(n) else s_cols
+            return slice(first + width - P, first + width)
+
+        def load_s_columns():
+            first = Q - len(LATE_UNITS) * P
+            nc.sync.dma_start(out=s_bf[:, :, 0:1], in_=s[first:Q].rearrange("(c n o) -> n c o", n=P, o=1))
+
+        def late_product(n):
+            second_product(take_bank(("zt", n))[:], slice(P * J, 2 * P * J), late_chunk(n), True)
+
+        def late_scale(n):
+            bank = bank_of(("zt", n))
+            nc.scalar.activation(
+                out=late_zt[n - 2 * GROUPS][:].rearrange("q (g j t) -> q g j t", g=GROUPS, j=J),
+                in_=bank[:].rearrange("q (j g t) -> q g j t", g=GROUPS, j=J),
+                func=COPY,
+                scale=s_col[:, units - 1 - n : units - n],
+            )
+            give_bank(("zt", n))
 
         def unit_product(n):
             bank = take_bank(("z", n))
             first, width = q_range(n)
             if late(n):
                 for g in range(GROUPS):
-                    q_cols = slice(first + width - P, first + width)
-                    second_product(bank[:, g * P : (g + 1) * P], late_codes, late_scales, g * P, q_cols)
+                    cols = slice(g * P, (g + 1) * P)
+                    nc.tensor.transpose(bank[:, cols], late_zt[n - 2 * GROUPS][:, cols], ident[:])
             else:
-                second_product(bank[:], x_codes, x_scales, (n % GROUPS) * P, slice(first, first + width))
+                g = n % GROUPS
+                second_product(bank[:], slice(g * P, (g + 1) * P), slice(first, first + width), False)
 
         def unit_copy(n):
             z = bank_of(("z", n))[:]
@@ -298,13 +310,16 @@ def tile_lokrrankgatedkroneckerdelta_w4_kernel(
         def unit_finish(n):
             bank = bank_of(("mixed", n))
             result = by_group(n, unit_out[n])
-            if n < UNITS_ON_GPSIMD:
-                nc.scalar.copy(out=result, in_=by_group(n, bank))
-                nc.gpsimd.tensor_tensor(out=result, in0=result, in1=s_for_unit(n), op=MULT)
-            else:
-                nc.vector.tensor_tensor(out=result, in0=by_group(n, bank), in1=s_for_unit(n), op=MULT)
-            give_bank(("mixed", n))
             first, width = q_range(n)
+            s_cols = s_all[:, first : first + width]
+            if late(n):
+                nc.scalar.copy(out=result, in_=by_group(n, bank))
+            elif n < UNITS_ON_GPSIMD:
+                nc.scalar.copy(out=result, in_=bank[:])
+                nc.gpsimd.tensor_tensor(out=result, in0=result, in1=s_cols, op=MULT)
+            else:
+                nc.vector.tensor_tensor(out=result, in0=bank[:], in1=s_cols, op=MULT)
+            give_bank(("mixed", n))
             if late(n):
                 dst = out_rows[P * J :, first : first + width].rearrange("(g n) q -> n g q", n=P)
             else:
@@ -313,7 +328,10 @@ def tile_lokrrankgatedkroneckerdelta_w4_kernel(
 
         def chain_product(half, j):
             bank = take_bank(("zj", half, j))
-            second_product(bank[:], x_codes, x_scales, (J + j) * P, slice(half * BANK, (half + 1) * BANK))
+            x_cols = slice((J + j) * P, (J + j + 1) * P)
+            for start, width in CHAIN_PASSES[half]:
+                q_cols = slice(half * BANK + start, half * BANK + start + width)
+                second_product(bank[:, start : start + width], x_cols, q_cols, False)
 
         def chain_term(n, j):
             half, i = chains[n]
@@ -349,6 +367,7 @@ def tile_lokrrankgatedkroneckerdelta_w4_kernel(
         scale_x(0)
         for t in range(1, PACK):
             quantize_be(t)
+        load_s_columns()
         nc.scalar.activation(out=a_all[:], in_=a_bf[:], func=COPY)
 
         scale_x(1)
@@ -392,27 +411,40 @@ def tile_lokrrankgatedkroneckerdelta_w4_kernel(
         copy_x(3, on_vector)
         quantize_x(1)
         copy_w2(5, on_scalar)
+        nc.scalar.activation(out=s_col[:], in_=s_bf[:, :, 0], func=COPY)
         unit_product(1)
         chain_product(0, 1)
         quantize_x(3)
         unit_copy(0)
         unit_mix(0)
         quantize(w2_late[:], w2_codes, w2_scales, BANK, BANK)
-        regroup_late_codes()
         unit_copy(1)
+        chain_product(0, 2)
+        chain_product(0, 3)
         chain_term(0, 0)
         chain_term(1, 0)
 
         for n in range(len(chains)):
-            if n + 2 < len(chains):
-                chain_product(*divmod(n + 2, J))
-            unit_product(n + 2)
+            if 2 <= n < 2 + J:
+                chain_product(1, n - 2)
+            if not late(n + 2):
+                unit_product(n + 2)
+            elif not late(n + 1):
+                for unit in range(n + 2, units):
+                    unit_product(unit)
+            if late(n + 4) and n + 4 < units:
+                late_product(n + 4)
             unit_mix(n + 1)
-            unit_finish(n)
+            if n < UNITS_ON_GPSIMD:
+                unit_finish(n)
             unit_copy(n + 2)
+            if late(n + 4) and n + 4 < units:
+                late_scale(n + 4)
             if n + 2 < len(chains):
                 chain_term(n + 2, 0)
             chain_term(n, 1)
+            if n >= UNITS_ON_GPSIMD:
+                unit_finish(n)
             if n > 0:
                 chain_term(n - 1, 3)
                 chain_finish(n - 1)

@@ -443,12 +443,12 @@ def tile_lokrrankgatedkroneckerdelta_w4_kernel(
             if n + 2 < len(chains):
                 chain_term(n + 2, 0)
             chain_term(n, 1)
-            if n >= UNITS_ON_GPSIMD:
-                unit_finish(n)
             if n > 0:
                 chain_term(n - 1, 3)
                 chain_finish(n - 1)
             chain_term(n, 2)
+            if n >= UNITS_ON_GPSIMD:
+                unit_finish(n)
         unit_mix(units - 1)
         unit_finish(units - 2)
         chain_term(len(chains) - 1, 3)

@@ -27,8 +27,10 @@ BANKS = 8
 GROUP = P // J
 GROUPS = P // GROUP
 
-LATE_UNITS = ((Q - P, P), (Q - P - 64, 64))
-CHAIN_RANGES = ((0, BANK), (BANK, LATE_UNITS[1][0] - BANK))
+LATE_UNIT = 2 * GROUPS
+UNITS = LATE_UNIT + 1
+LATE_Q = Q - P
+CHAIN_RANGES = ((0, BANK), (BANK, LATE_Q - BANK))
 CHAIN_PASSES = (((0, BANK),), ((0, 2 * P), (2 * P, P)))
 UNITS_ON_GPSIMD = 3
 
@@ -78,30 +80,29 @@ def tile_lokrrankgatedkroneckerdelta_w4_kernel(
         be_codes = new("be_codes", [P, KP], U32)
         be_scales = new("be_scales", [P, KP], U8)
         c_codes = new("c_codes", [P, 2 * Q], U8)
-        c_plane = new("c_plane", [P, Q], U8)
-        x_raw = [new("x_raw%d" % half, [P, J, KP], U8) for half in range(2)]
+        c_scale_rows = new("c_scale_rows", [P, Q], U8)
+        x_raw = [new("x_raw%d" % n, [P, J, KP], U8) for n in range(T // P)]
         x_rows = [new("x_rows%d" % n, [P, KP], BF16) for n in range(2 * J)]
         x_turned_matrix = new("x_turned_matrix", [P, J * KP], BF16)
         x_turned_chain = [new("x_turned_chain%d" % n, [P, 2 * KP], BF16) for n in range(2)]
         x_codes = new("x_codes", [P, T * J], U32)
         x_scales = new("x_scales", [P, T * J], U8)
-        s_bf = new("s_bf", [P, len(LATE_UNITS), 2], BF16)
-        s_col = new("s_col", [P, len(LATE_UNITS)], F32)
-        late_zt = [new("late_zt%d" % n, [P, BANK], F32) for n in range(len(LATE_UNITS))]
-        w2_early = [new("w2_early%d" % n, [P, 2 * BANK], BF16) for n in range(2)]
-        w2_late = new("w2_late", [P, 4 * BANK], BF16)
+        s_late_bf = new("s_late_bf", [P, 1], BF16)
+        s_late = new("s_late", [P, 1], F32)
+        late_turned = new("late_turned", [P, BANK], F32)
+        w2_first = [new("w2_first%d" % n, [P, 2 * BANK], BF16) for n in range(2)]
+        w2_second = new("w2_second", [P, 4 * BANK], BF16)
         w2_codes = new("w2_codes", [P, Q], U32)
         w2_scales = new("w2_scales", [P, Q], U8)
-        units = 2 * GROUPS + len(LATE_UNITS)
-        unit_z = [new("unit_z%d" % n, [P, BANK], F32) for n in range(units)]
-        unit_out = [new("unit_out%d" % n, [P, BANK], F32) for n in range(units)]
+        unit_z = [new("unit_z%d" % n, [P, BANK], F32) for n in range(UNITS)]
+        unit_out = [new("unit_out%d" % n, [P, BANK], F32) for n in range(UNITS)]
         chains = [(half, i) for half in range(2) for i in range(J)]
         chain_sum = [new("chain_sum%d" % n, [P, CHAIN_RANGES[n // J][1]], F32) for n in range(len(chains))]
 
         make_identity(nc, ident[:])
         ctx.enter_context(tc.manual_schedule(engines=set([ENGINE.PE, ENGINE.Activation, ENGINE.DVE, ENGINE.Pool])))
 
-        nc.vector.memset(c_plane[:].bitcast(I32), 0)
+        nc.vector.memset(c_scale_rows[:].bitcast(I32), 0)
         nc.sync.dma_start(out=e_pairs[:], in_=e.rearrange("(w n k) -> n w k", n=P, k=2))
         nc.scalar.dma_start(out=xs_col[:], in_=x_scale.rearrange("o u (n m) -> n (o u m)", m=PACK))
         nc.scalar.dma_start(out=a_bf[:], in_=a.rearrange("i j -> (i j)").partition_broadcast(P))
@@ -109,18 +110,18 @@ def tile_lokrrankgatedkroneckerdelta_w4_kernel(
             nc.sync.dma_start(out=b_rows[t][:], in_=b.rearrange("(m t) r -> m t r", t=PACK)[:, t, :])
         nc.sync.dma_start(out=x_raw[0][:], in_=x_bytes[0:P])
         nc.sync.dma_start(out=c_codes[:].bitcast(I32), in_=c_words[0].bitcast(I32))
-        for g in range(4):
+        for quad in range(P // 32):
             nc.sync.dma_start(
-                out=c_plane[32 * g : 32 * g + 4, :].bitcast(I32),
-                in_=c_scales[0, 4 * g : 4 * g + 4, :].bitcast(I32),
+                out=c_scale_rows[32 * quad : 32 * quad + 4, :].bitcast(I32),
+                in_=c_scales[0, 4 * quad : 4 * quad + 4, :].bitcast(I32),
             )
         nc.sync.dma_start(out=x_raw[1][:], in_=x_bytes[P : 2 * P])
 
         nc.vector.tensor_reduce(
-            out=same_block[:], in_=ident[:].rearrange("n (j t) -> n j t", j=J), axis=AXIS_X, op=ADD
+            out=same_block[:], in_=ident[:].rearrange("n (j tok) -> n j tok", j=J), axis=AXIS_X, op=ADD
         )
         nc.vector.tensor_reduce(
-            out=same_token[:], in_=ident[:].rearrange("n (j t) -> n t j", j=J), axis=AXIS_X, op=ADD
+            out=same_token[:], in_=ident[:].rearrange("n (j tok) -> n tok j", j=J), axis=AXIS_X, op=ADD
         )
 
         def spread(bank, columns, count):
@@ -151,7 +152,7 @@ def tile_lokrrankgatedkroneckerdelta_w4_kernel(
 
         def build_mixer():
             nc.vector.tensor_tensor(
-                out=mixer[:].rearrange("n (t i) -> n t i", i=J),
+                out=mixer[:].rearrange("n (tok i) -> n tok i", i=J),
                 in0=same_token[:].unsqueeze(2).to_broadcast([P, GROUP, J]),
                 in1=a_col[:].unsqueeze(1).to_broadcast([P, GROUP, J]),
                 op=MULT,
@@ -191,21 +192,21 @@ def tile_lokrrankgatedkroneckerdelta_w4_kernel(
                     lhsT=be_codes[:, t * P : (t + 1) * P].bitcast(FP8X4),
                     lhsT_scale=be_scales[:, t * P : (t + 1) * P],
                     rhs=c_codes[:, 2 * c * P : 2 * (c + 1) * P].bitcast(FP4X4),
-                    rhs_scale=c_plane[:, c * P : (c + 1) * P],
+                    rhs_scale=c_scale_rows[:, c * P : (c + 1) * P],
                     start=True,
                     stop=True,
                 )
 
         def copy_w2(c, copy):
-            wide, slot = (w2_early[c // 2], c % 2) if c < 4 else (w2_late, c - 4)
+            wide, slot = (w2_first[c // 2], c % 2) if c < 4 else (w2_second, c - 4)
             copy(
                 out=wide[:, slot * BANK : (slot + 1) * BANK].rearrange("m (q t) -> m q t", t=PACK),
                 in_=bank_of(("w2", c))[:].rearrange("m (t q) -> m q t", t=PACK),
             )
             give_bank(("w2", c))
 
-        def quantize_w2_early(n):
-            quantize(w2_early[n][:], w2_codes, w2_scales, 2 * n * P, 2 * P)
+        def quantize_w2_first(n):
+            quantize(w2_first[n][:], w2_codes, w2_scales, 2 * n * P, 2 * P)
 
         def scale_x(n):
             nc.vector.tensor_tensor(
@@ -220,15 +221,16 @@ def tile_lokrrankgatedkroneckerdelta_w4_kernel(
         def copy_x(pair, copy):
             bank = bank_of(("x", pair))
             if pair < 2:
-                wide = x_turned_matrix[:].bitcast(F32).rearrange("n (g j t u) -> n j g t u", g=GROUPS, j=J, u=2)
+                words = x_turned_matrix[:].bitcast(F32)
+                wide = words.rearrange("n (g j tok u) -> n j g tok u", g=GROUPS, j=J, u=2)
                 copy(
                     out=wide[:, 2 * pair : 2 * pair + 2],
-                    in_=bank[:].rearrange("n (j u g t) -> n j g t u", j=2, u=2, g=GROUPS),
+                    in_=bank[:].rearrange("n (j u g tok) -> n j g tok u", j=2, u=2, g=GROUPS),
                 )
             else:
                 copy(
-                    out=x_turned_chain[pair - 2][:].bitcast(F32).rearrange("n (j t u) -> n j t u", j=2, u=2),
-                    in_=bank[:].rearrange("n (j u t) -> n j t u", j=2, u=2),
+                    out=x_turned_chain[pair - 2][:].bitcast(F32).rearrange("n (j tok u) -> n j tok u", j=2, u=2),
+                    in_=bank[:].rearrange("n (j u tok) -> n j tok u", j=2, u=2),
                 )
             give_bank(("x", pair))
 
@@ -250,81 +252,57 @@ def tile_lokrrankgatedkroneckerdelta_w4_kernel(
                 stop=True,
             )
 
-        out_rows = out.rearrange("t i q -> (t i) q")
+        out_rows = out.rearrange("tok i q -> (tok i) q")
 
-        def late(n):
-            return n >= 2 * GROUPS
+        def late_product():
+            second_product(take_bank("late")[:], slice(P * J, 2 * P * J), slice(LATE_Q, Q), True)
 
-        def q_range(n):
-            return LATE_UNITS[n - 2 * GROUPS] if late(n) else ((n // GROUPS) * BANK, BANK)
-
-        def flat(n, buffer):
-            return buffer[:, 0 : GROUPS * q_range(n)[1]] if late(n) else buffer[:]
-
-        def by_group(n, buffer):
-            return flat(n, buffer).rearrange("n (g q) -> n g q", g=GROUPS) if late(n) else buffer[:]
-
-        def late_chunk(n):
-            first, width = q_range(n)
-            return slice(first + width - P, first + width)
-
-        def load_s_columns():
-            first = Q - len(LATE_UNITS) * P
-            nc.sync.dma_start(out=s_bf[:, :, 0:1], in_=s[first:Q].rearrange("(c n o) -> n c o", n=P, o=1))
-
-        def late_product(n):
-            second_product(take_bank(("zt", n))[:], slice(P * J, 2 * P * J), late_chunk(n), True)
-
-        def late_scale(n):
-            bank = bank_of(("zt", n))
+        def late_scale():
             nc.scalar.activation(
-                out=late_zt[n - 2 * GROUPS][:].rearrange("q (g j t) -> q g j t", g=GROUPS, j=J),
-                in_=bank[:].rearrange("q (j g t) -> q g j t", g=GROUPS, j=J),
+                out=late_turned[:].rearrange("q (g j tok) -> q g j tok", g=GROUPS, j=J),
+                in_=bank_of("late")[:].rearrange("q (j g tok) -> q g j tok", g=GROUPS, j=J),
                 func=COPY,
-                scale=s_col[:, units - 1 - n : units - n],
+                scale=s_late[:],
             )
-            give_bank(("zt", n))
+            give_bank("late")
 
         def unit_product(n):
             bank = take_bank(("z", n))
-            first, width = q_range(n)
-            if late(n):
+            if n == LATE_UNIT:
                 for g in range(GROUPS):
                     cols = slice(g * P, (g + 1) * P)
-                    nc.tensor.transpose(bank[:, cols], late_zt[n - 2 * GROUPS][:, cols], ident[:])
+                    nc.tensor.transpose(bank[:, cols], late_turned[:, cols], ident[:])
             else:
-                g = n % GROUPS
-                second_product(bank[:], slice(g * P, (g + 1) * P), slice(first, first + width), False)
+                half, g = divmod(n, GROUPS)
+                second_product(bank[:], slice(g * P, (g + 1) * P), slice(half * BANK, (half + 1) * BANK), False)
 
         def unit_copy(n):
-            z = bank_of(("z", n))[:]
-            if late(n):
-                z = z.rearrange("n (g q) -> n g q", g=GROUPS)[:, :, P - q_range(n)[1] :]
-            nc.scalar.copy(out=by_group(n, unit_z[n]), in_=z)
+            nc.scalar.copy(out=unit_z[n][:], in_=bank_of(("z", n))[:])
             give_bank(("z", n))
 
         def unit_mix(n):
-            bank = take_bank(("mixed", n))
-            nc.tensor.matmul(flat(n, bank), lhsT=mixer[:], rhs=flat(n, unit_z[n]), start=True, stop=True)
+            nc.tensor.matmul(take_bank(("mixed", n))[:], lhsT=mixer[:], rhs=unit_z[n][:], start=True, stop=True)
 
         def unit_finish(n):
             bank = bank_of(("mixed", n))
-            result = by_group(n, unit_out[n])
-            first, width = q_range(n)
-            s_cols = s_all[:, first : first + width]
-            if late(n):
-                nc.scalar.copy(out=result, in_=by_group(n, bank))
-            elif n < UNITS_ON_GPSIMD:
+            result = unit_out[n][:]
+            if n == LATE_UNIT:
                 nc.scalar.copy(out=result, in_=bank[:])
-                nc.gpsimd.tensor_tensor(out=result, in0=result, in1=s_cols, op=MULT)
+                give_bank(("mixed", n))
+                nc.sync.dma_start(
+                    out=out_rows[P * J :, LATE_Q:].rearrange("(g n) q -> n g q", n=P),
+                    in_=result.rearrange("n (g q) -> n g q", g=GROUPS),
+                )
+                return
+            half, g = divmod(n, GROUPS)
+            q_cols = slice(half * BANK, (half + 1) * BANK)
+            if n < UNITS_ON_GPSIMD:
+                nc.scalar.copy(out=result, in_=bank[:])
+                nc.gpsimd.tensor_tensor(out=result, in0=result, in1=s_all[:, q_cols], op=MULT)
             else:
-                nc.vector.tensor_tensor(out=result, in0=bank[:], in1=s_cols, op=MULT)
+                nc.vector.tensor_tensor(out=result, in0=bank[:], in1=s_all[:, q_cols], op=MULT)
             give_bank(("mixed", n))
-            if late(n):
-                dst = out_rows[P * J :, first : first + width].rearrange("(g n) q -> n g q", n=P)
-            else:
-                dst = out_rows[(n % GROUPS) * P : (n % GROUPS + 1) * P, first : first + width]
-            nc.sync.dma_start(out=dst, in_=result)
+            nc.sync.dma_start(out=out_rows[g * P : (g + 1) * P, q_cols], in_=result)
 
         def chain_product(half, j):
             bank = take_bank(("zj", half, j))
@@ -367,7 +345,7 @@ def tile_lokrrankgatedkroneckerdelta_w4_kernel(
         scale_x(0)
         for t in range(1, PACK):
             quantize_be(t)
-        load_s_columns()
+        nc.sync.dma_start(out=s_late_bf[:], in_=s[LATE_Q:Q].rearrange("(n o) -> n o", o=1))
         nc.scalar.activation(out=a_all[:], in_=a_bf[:], func=COPY)
 
         scale_x(1)
@@ -384,7 +362,7 @@ def tile_lokrrankgatedkroneckerdelta_w4_kernel(
         turn_x(1)
         scale_x(4)
         copy_x(0, on_scalar)
-        quantize_w2_early(0)
+        quantize_w2_first(0)
         scale_x(5)
         copy_w2(2, on_scalar)
         copy_w2(3, on_scalar)
@@ -394,7 +372,7 @@ def tile_lokrrankgatedkroneckerdelta_w4_kernel(
         scale_x(6)
         build_mixer()
         copy_x(1, on_scalar)
-        quantize_w2_early(1)
+        quantize_w2_first(1)
         scale_x(7)
         copy_x(2, on_scalar)
 
@@ -411,35 +389,34 @@ def tile_lokrrankgatedkroneckerdelta_w4_kernel(
         copy_x(3, on_vector)
         quantize_x(1)
         copy_w2(5, on_scalar)
-        nc.scalar.activation(out=s_col[:], in_=s_bf[:, :, 0], func=COPY)
+        nc.scalar.activation(out=s_late[:], in_=s_late_bf[:], func=COPY)
         unit_product(1)
         chain_product(0, 1)
         quantize_x(3)
         unit_copy(0)
         unit_mix(0)
-        quantize(w2_late[:], w2_codes, w2_scales, BANK, BANK)
+        quantize(w2_second[:], w2_codes, w2_scales, BANK, BANK)
         unit_copy(1)
         chain_product(0, 2)
         chain_product(0, 3)
         chain_term(0, 0)
         chain_term(1, 0)
 
+        late_round = (LATE_UNIT - 2) - 2
         for n in range(len(chains)):
             if 2 <= n < 2 + J:
                 chain_product(1, n - 2)
-            if not late(n + 2):
+            if n + 2 < UNITS:
                 unit_product(n + 2)
-            elif not late(n + 1):
-                for unit in range(n + 2, units):
-                    unit_product(unit)
-            if late(n + 4) and n + 4 < units:
-                late_product(n + 4)
+            if n == late_round:
+                late_product()
             unit_mix(n + 1)
             if n < UNITS_ON_GPSIMD:
                 unit_finish(n)
-            unit_copy(n + 2)
-            if late(n + 4) and n + 4 < units:
-                late_scale(n + 4)
+            if n + 2 < UNITS:
+                unit_copy(n + 2)
+            if n == late_round:
+                late_scale()
             if n + 2 < len(chains):
                 chain_term(n + 2, 0)
             chain_term(n, 1)
@@ -449,8 +426,6 @@ def tile_lokrrankgatedkroneckerdelta_w4_kernel(
             chain_term(n, 2)
             if n >= UNITS_ON_GPSIMD:
                 unit_finish(n)
-        unit_mix(units - 1)
-        unit_finish(units - 2)
         chain_term(len(chains) - 1, 3)
-        unit_finish(units - 1)
+        unit_finish(LATE_UNIT)
         chain_finish(len(chains) - 1)

from contextlib import ExitStack

import concourse.mybir as mybir
from concourse.masks import make_identity

T, J, KP, R, Q = 256, 4, 512, 512, 1024
FLOPS = 2 * KP * R * Q + 2 * T * J * KP * Q + 2 * T * J * J * Q

F32 = mybir.dt.float32
BF16 = mybir.dt.bfloat16
I32 = mybir.dt.int32
U32 = mybir.dt.uint32
U8 = mybir.dt.uint8
FP8 = mybir.dt.float8_e4m3fn
FP8X4 = mybir.dt.float8_e4m3fn_x4
FP4X4 = mybir.dt.float4_e2m1fn_x4
MULT = mybir.AluOpType.mult
ADD = mybir.AluOpType.add
COPY = mybir.ActivationFunctionType.Copy
AXIS_X = mybir.AxisListType.X
ENGINE = mybir.EngineType

P = 128
PACK = 4
BANK = 512
BANKS = 8
GROUP = P // J
GROUPS = P // GROUP

LATE_UNIT = 2 * GROUPS
UNITS = LATE_UNIT + 1
LATE_Q = Q - P
CHAIN_RANGES = ((0, BANK), (BANK, LATE_Q - BANK))
CHAIN_PASSES = (((0, BANK),), ((0, 2 * P), (2 * P, P)))
UNITS_ON_GPSIMD = 3


def tile_lokrrankgatedkroneckerdelta_w4_kernel(
    tc, x_bytes, x_scale, a, b, e, c_words, c_scales, s, out
):
    nc = tc.nc
    with ExitStack() as ctx:
        sbuf = ctx.enter_context(tc.tile_pool(name="sbuf", bufs=1))
        psum = ctx.enter_context(tc.psum_pool(name="psum", bufs=1))

        def new(name, shape, dtype):
            return sbuf.tile(shape, dtype, name=name, align_bytes=64)

        free_banks = list(range(BANKS))
        held = {}

        def take_bank(use):
            number = free_banks[0]
            free_banks.remove(number)
            bank = psum.tile([P, BANK], F32, name="bank%d" % number, tag="bank%d" % number)
            held.setdefault(use, (number, bank))
            return bank

        def bank_of(use):
            return held[use][1]

        def give_bank(use):
            free_banks.append(held[use][0])

        ident = new("ident", [P, P], F32)
        same_token = new("same_token", [P, GROUP], F32)
        same_block = new("same_block", [P, J], F32)
        a_bf = new("a_bf", [P, J * J], BF16)
        a_all = new("a_all", [P, J * J], F32)
        a_masked = new("a_masked", [P, J, J], F32)
        a_col = new("a_col", [P, J], F32)
        mixer = new("mixer", [P, P], F32)
        e_pairs = new("e_pairs", [P, 2, 2], BF16)
        xs_col = new("xs_col", [P, PACK], F32)
        xs_all = new("xs_all", [P, KP], F32)
        s_all = new("s_all", [P, Q], BF16)
        b_rows = [new("b_rows%d" % t, [P, R], BF16) for t in range(PACK)]
        be_rows = [new("be_rows%d" % t, [P, R], BF16) for t in range(PACK)]
        be_turned = [new("be_turned%d" % t, [P, R], BF16) for t in range(PACK)]
        be_codes = new("be_codes", [P, KP], U32)
        be_scales = new("be_scales", [P, KP], U8)
        c_codes = new("c_codes", [P, 2 * Q], U8)
        c_scale_rows = new("c_scale_rows", [P, Q], U8)
        x_raw = [new("x_raw%d" % n, [P, J, KP], U8) for n in range(T // P)]
        x_rows = [new("x_rows%d" % n, [P, KP], BF16) for n in range(2 * J)]
        x_turned_matrix = new("x_turned_matrix", [P, J * KP], BF16)
        x_turned_chain = [new("x_turned_chain%d" % n, [P, 2 * KP], BF16) for n in range(2)]
        x_codes = new("x_codes", [P, T * J], U32)
        x_scales = new("x_scales", [P, T * J], U8)
        s_late_bf = new("s_late_bf", [P, 1], BF16)
        s_late = new("s_late", [P, 1], F32)
        late_turned = new("late_turned", [P, BANK], F32)
        w2_first = [new("w2_first%d" % n, [P, 2 * BANK], BF16) for n in range(2)]
        w2_second = new("w2_second", [P, 4 * BANK], BF16)
        w2_codes = new("w2_codes", [P, Q], U32)
        w2_scales = new("w2_scales", [P, Q], U8)
        unit_z = [new("unit_z%d" % n, [P, BANK], F32) for n in range(UNITS)]
        unit_out = [new("unit_out%d" % n, [P, BANK], F32) for n in range(UNITS)]
        chains = [(half, i) for half in range(2) for i in range(J)]
        chain_sum = [new("chain_sum%d" % n, [P, CHAIN_RANGES[n // J][1]], F32) for n in range(len(chains))]

        make_identity(nc, ident[:])
        ctx.enter_context(tc.manual_schedule(engines=set([ENGINE.PE, ENGINE.Activation, ENGINE.DVE, ENGINE.Pool])))

        nc.vector.memset(c_scale_rows[:].bitcast(I32), 0)
        nc.sync.dma_start(out=e_pairs[:], in_=e.rearrange("(w n k) -> n w k", n=P, k=2))
        nc.scalar.dma_start(out=xs_col[:], in_=x_scale.rearrange("o u (n m) -> n (o u m)", m=PACK))
        nc.scalar.dma_start(out=a_bf[:], in_=a.rearrange("i j -> (i j)").partition_broadcast(P))
        for t in range(PACK):
            nc.sync.dma_start(out=b_rows[t][:], in_=b.rearrange("(m t) r -> m t r", t=PACK)[:, t, :])
        nc.sync.dma_start(out=x_raw[0][:], in_=x_bytes[0:P])
        nc.sync.dma_start(out=c_codes[:].bitcast(I32), in_=c_words[0].bitcast(I32))
        for quad in range(P // 32):
            nc.sync.dma_start(
                out=c_scale_rows[32 * quad : 32 * quad + 4, :].bitcast(I32),
                in_=c_scales[0, 4 * quad : 4 * quad + 4, :].bitcast(I32),
            )
        nc.sync.dma_start(out=x_raw[1][:], in_=x_bytes[P : 2 * P])

        nc.vector.tensor_reduce(
            out=same_block[:], in_=ident[:].rearrange("n (j tok) -> n j tok", j=J), axis=AXIS_X, op=ADD
        )
        nc.vector.tensor_reduce(
            out=same_token[:], in_=ident[:].rearrange("n (j tok) -> n tok j", j=J), axis=AXIS_X, op=ADD
        )

        def spread(bank, columns, count):
            for m in range(count):
                nc.tensor.transpose(
                    bank[:, m * P : (m + 1) * P], columns[:, m : m + 1].to_broadcast([P, P]), ident[:]
                )

        spread(take_bank("e"), e_pairs[:].rearrange("n w k -> n (w k)").bitcast(F32), 2)
        spread(take_bank("xs"), xs_col[:], PACK)
        nc.scalar.activation(
            out=xs_all[:].rearrange("n (k m) -> n k m", m=PACK),
            in_=bank_of("xs")[:].rearrange("n (m k) -> n k m", m=PACK),
            func=COPY,
        )
        give_bank("xs")

        def mask_a():
            nc.vector.tensor_tensor(
                out=a_masked[:],
                in0=a_bf[:].rearrange("n (i j) -> n i j", j=J),
                in1=same_block[:].unsqueeze(1).to_broadcast([P, J, J]),
                op=MULT,
            )

        def pick_a():
            nc.vector.tensor_reduce(out=a_col[:], in_=a_masked[:], axis=AXIS_X, op=ADD)

        def build_mixer():
            nc.vector.tensor_tensor(
                out=mixer[:].rearrange("n (tok i) -> n tok i", i=J),
                in0=same_token[:].unsqueeze(2).to_broadcast([P, GROUP, J]),
                in1=a_col[:].unsqueeze(1).to_broadcast([P, GROUP, J]),
                op=MULT,
            )

        def turn(rows, bank, slot):
            words = rows[:].bitcast(F32)
            for u in range(2):
                first = (2 * slot + u) * P
                nc.tensor.transpose(bank[:, first : first + P], words[:, u : 2 * P : 2], ident[:])

        def quantize(src, codes, scales, first, count):
            nc.vector.quantize_mx(
                out=codes[:, first : first + count].bitcast(FP8X4), scales=scales[:, first : first + count], in_=src
            )

        def gate_and_turn_b(t):
            nc.vector.tensor_tensor(
                out=be_rows[t][:], in0=b_rows[t][:], in1=bank_of("e")[:, 0 : R // 2].bitcast(BF16), op=MULT
            )
            bank = take_bank(("be", t))
            turn(be_rows[t], bank, 0)
            nc.scalar.copy(
                out=be_turned[t][:].bitcast(F32).rearrange("n (m u) -> n m u", u=2),
                in_=bank[:, 0 : 2 * P].rearrange("n (u m) -> n m u", u=2),
            )
            give_bank(("be", t))

        def quantize_be(t):
            quantize(be_turned[t][:], be_codes, be_scales, t * P, P)

        def make_w2(c):
            bank = take_bank(("w2", c))
            for t in range(PACK):
                nc.tensor.matmul_mx(
                    out=bank[:, t * P : (t + 1) * P],
                    lhsT=be_codes[:, t * P : (t + 1) * P].bitcast(FP8X4),
                    lhsT_scale=be_scales[:, t * P : (t + 1) * P],
                    rhs=c_codes[:, 2 * c * P : 2 * (c + 1) * P].bitcast(FP4X4),
                    rhs_scale=c_scale_rows[:, c * P : (c + 1) * P],
                    start=True,
                    stop=True,
                )

        def copy_w2(c, copy):
            wide, slot = (w2_first[c // 2], c % 2) if c < 4 else (w2_second, c - 4)
            copy(
                out=wide[:, slot * BANK : (slot + 1) * BANK].rearrange("m (q t) -> m q t", t=PACK),
                in_=bank_of(("w2", c))[:].rearrange("m (t q) -> m q t", t=PACK),
            )
            give_bank(("w2", c))

        def quantize_w2_first(n):
            quantize(w2_first[n][:], w2_codes, w2_scales, 2 * n * P, 2 * P)

        def scale_x(n):
            nc.vector.tensor_tensor(
                out=x_rows[n][:], in0=x_raw[n // J][:, n % J, :].bitcast(FP8), in1=xs_all[:], op=MULT
            )

        def turn_x(pair):
            bank = take_bank(("x", pair))
            for slot in range(2):
                turn(x_rows[2 * pair + slot], bank, slot)

        def copy_x(pair, copy):
            bank = bank_of(("x", pair))
            if pair < 2:
                words = x_turned_matrix[:].bitcast(F32)
                wide = words.rearrange("n (g j tok u) -> n j g tok u", g=GROUPS, j=J, u=2)
                copy(
                    out=wide[:, 2 * pair : 2 * pair + 2],
                    in_=bank[:].rearrange("n (j u g tok) -> n j g tok u", j=2, u=2, g=GROUPS),
                )
            else:
                copy(
                    out=x_turned_chain[pair - 2][:].bitcast(F32).rearrange("n (j tok u) -> n j tok u", j=2, u=2),
                    in_=bank[:].rearrange("n (j u tok) -> n j tok u", j=2, u=2),
                )
            give_bank(("x", pair))

        def quantize_x(n):
            src = x_turned_matrix[:, 2 * n * KP : 2 * (n + 1) * KP] if n < 2 else x_turned_chain[n - 2][:]
            quantize(src, x_codes, x_scales, 2 * n * P, 2 * P)

        def second_product(dst, x_cols, q_cols, turned):
            x_part = (x_codes[:, x_cols].bitcast(FP8X4), x_scales[:, x_cols])
            w2_part = (w2_codes[:, q_cols].bitcast(FP8X4), w2_scales[:, q_cols])
            stationary, moving = (w2_part, x_part) if turned else (x_part, w2_part)
            nc.tensor.matmul_mx(
                out=dst,
                lhsT=stationary[0],
                lhsT_scale=stationary[1],
                rhs=moving[0],
                rhs_scale=moving[1],
                start=True,
                stop=True,
            )

        out_rows = out.rearrange("tok i q -> (tok i) q")

        def late_product():
            second_product(take_bank("late")[:], slice(P * J, 2 * P * J), slice(LATE_Q, Q), True)

        def late_scale():
            nc.scalar.activation(
                out=late_turned[:].rearrange("q (g j tok) -> q g j tok", g=GROUPS, j=J),
                in_=bank_of("late")[:].rearrange("q (j g tok) -> q g j tok", g=GROUPS, j=J),
                func=COPY,
                scale=s_late[:],
            )
            give_bank("late")

        def unit_product(n):
            bank = take_bank(("z", n))
            if n == LATE_UNIT:
                for g in range(GROUPS):
                    cols = slice(g * P, (g + 1) * P)
                    nc.tensor.transpose(bank[:, cols], late_turned[:, cols], ident[:])
            else:
                half, g = divmod(n, GROUPS)
                second_product(bank[:], slice(g * P, (g + 1) * P), slice(half * BANK, (half + 1) * BANK), False)

        def unit_copy(n):
            nc.scalar.copy(out=unit_z[n][:], in_=bank_of(("z", n))[:])
            give_bank(("z", n))

        def unit_mix(n):
            nc.tensor.matmul(take_bank(("mixed", n))[:], lhsT=mixer[:], rhs=unit_z[n][:], start=True, stop=True)

        def unit_finish(n):
            bank = bank_of(("mixed", n))
            result = unit_out[n][:]
            if n == LATE_UNIT:
                nc.scalar.copy(out=result, in_=bank[:])
                give_bank(("mixed", n))
                nc.sync.dma_start(
                    out=out_rows[P * J :, LATE_Q:].rearrange("(g n) q -> n g q", n=P),
                    in_=result.rearrange("n (g q) -> n g q", g=GROUPS),
                )
                return
            half, g = divmod(n, GROUPS)
            q_cols = slice(half * BANK, (half + 1) * BANK)
            if n < UNITS_ON_GPSIMD:
                nc.scalar.copy(out=result, in_=bank[:])
                nc.gpsimd.tensor_tensor(out=result, in0=result, in1=s_all[:, q_cols], op=MULT)
            else:
                nc.vector.tensor_tensor(out=result, in0=bank[:], in1=s_all[:, q_cols], op=MULT)
            give_bank(("mixed", n))
            nc.sync.dma_start(out=out_rows[g * P : (g + 1) * P, q_cols], in_=result)

        def chain_product(half, j):
            bank = take_bank(("zj", half, j))
            x_cols = slice((J + j) * P, (J + j + 1) * P)
            for start, width in CHAIN_PASSES[half]:
                q_cols = slice(half * BANK + start, half * BANK + start + width)
                second_product(bank[:, start : start + width], x_cols, q_cols, False)

        def chain_term(n, j):
            half, i = chains[n]
            z = bank_of(("zj", half, j))[:, 0 : CHAIN_RANGES[half][1]]
            weight = a_all[:, J * i + j : J * i + j + 1]
            if j == 0:
                nc.scalar.activation(out=chain_sum[n][:], in_=z, func=COPY, scale=weight)
            else:
                nc.vector.scalar_tensor_tensor(
                    out=chain_sum[n][:], in0=z, scalar=weight, in1=chain_sum[n][:], op0=MULT, op1=ADD
                )
            if i == J - 1:
                give_bank(("zj", half, j))

        def chain_finish(n):
            half, i = chains[n]
            first, width = CHAIN_RANGES[half]
            engine = nc.vector if n == len(chains) - 1 else nc.gpsimd
            engine.tensor_tensor(
                out=chain_sum[n][:], in0=chain_sum[n][:], in1=s_all[:, first : first + width], op=MULT
            )
            nc.sync.dma_start(out=out[P : 2 * P, i, first : first + width], in_=chain_sum[n][:])

        on_scalar = nc.scalar.copy
        on_vector = nc.vector.tensor_copy

        for t in range(PACK):
            gate_and_turn_b(t)
        give_bank("e")
        mask_a()
        quantize_be(0)
        pick_a()
        scale_x(0)
        for t in range(1, PACK):
            quantize_be(t)
        nc.sync.dma_start(out=s_late_bf[:], in_=s[LATE_Q:Q].rearrange("(n o) -> n o", o=1))
        nc.scalar.activation(out=a_all[:], in_=a_bf[:], func=COPY)

        scale_x(1)
        make_w2(0)
        make_w2(1)
        turn_x(0)
        make_w2(2)
        make_w2(3)
        scale_x(2)
        scale_x(3)
        copy_w2(0, on_scalar)
        copy_w2(1, on_scalar)
        nc.scalar.dma_start(out=s_all[:], in_=s.partition_broadcast(P))
        turn_x(1)
        scale_x(4)
        copy_x(0, on_scalar)
        quantize_w2_first(0)
        scale_x(5)
        copy_w2(2, on_scalar)
        copy_w2(3, on_scalar)
        turn_x(2)
        make_w2(4)
        make_w2(5)
        scale_x(6)
        build_mixer()
        copy_x(1, on_scalar)
        quantize_w2_first(1)
        scale_x(7)
        copy_x(2, on_scalar)

        make_w2(6)
        make_w2(7)
        quantize_x(0)
        turn_x(3)
        quantize_x(2)
        copy_w2(4, on_scalar)
        copy_w2(6, on_vector)
        unit_product(0)
        chain_product(0, 0)
        copy_w2(7, on_vector)
        copy_x(3, on_vector)
        quantize_x(1)
        copy_w2(5, on_scalar)
        nc.scalar.activation(out=s_late[:], in_=s_late_bf[:], func=COPY)
        unit_product(1)
        chain_product(0, 1)
        quantize_x(3)
        unit_copy(0)
        unit_mix(0)
        quantize(w2_second[:], w2_codes, w2_scales, BANK, BANK)
        unit_copy(1)
        chain_product(0, 2)
        chain_product(0, 3)
        chain_term(0, 0)
        chain_term(1, 0)

        late_round = (LATE_UNIT - 2) - 2
        for n in range(len(chains)):
            if 2 <= n < 2 + J:
                chain_product(1, n - 2)
            if n + 2 < UNITS:
                unit_product(n + 2)
            if n == late_round:
                late_product()
            unit_mix(n + 1)
            if n < UNITS_ON_GPSIMD:
                unit_finish(n)
            if n + 2 < UNITS:
                unit_copy(n + 2)
            if n == late_round:
                late_scale()
            if n + 2 < len(chains):
                chain_term(n + 2, 0)
            chain_term(n, 1)
            if n > 0:
                chain_term(n - 1, 3)
                chain_finish(n - 1)
            chain_term(n, 2)
            if n >= UNITS_ON_GPSIMD:
                unit_finish(n)
        chain_term(len(chains) - 1, 3)
        unit_finish(LATE_UNIT)
        chain_finish(len(chains) - 1)
